import numpy as np, ml_dtypes
CORES = [35,38,43,46]
N = 4
import mx_ref
BF = ml_dtypes.bfloat16
def gcols(t, e):
    v = np.concatenate([t.reshape(8, 16, -1, 4), np.zeros((8, 16, 1, 4), BF)], axis=2)
    return np.ascontiguousarray(np.stack([v[g][:, e[g]] for g in range(8)])).reshape(128, -1)
def tile(rs):
    return np.stack(rs, axis=2).reshape(128, -1).astype(BF)
def cut(t, i, w=512):
    return t[:, w * i:w * i + w]
def pick(q, e):
    c = np.concatenate([q[0].reshape(128, -1, 4), np.zeros((128, 1, 4), np.uint8)], axis=1); s = np.concatenate([q[1], np.ones((16, 1), np.uint8)], axis=1)
    return (np.ascontiguousarray(c[:, e].reshape(128, -1)), np.ascontiguousarray(s[:, e]))
def join(*qs):
    return (np.concatenate([q[0] for q in qs], axis=1), np.concatenate([q[1] for q in qs], axis=1))
def put(q, e, v):
    c, s = q[0].reshape(128, -1, 4).copy(), q[1].copy(); c[:, e] = v[0].reshape(128, -1, 4); s[:, e] = v[1]
    return (c.reshape(128, -1), s)
def pk(c, s):
    return (np.ascontiguousarray(c), mx_ref.live(s))
def emit(q):
    return q[0], q[1]
def packed(v, rng):
    q = [mx_ref.quantize(np.ascontiguousarray(v[r])) for r in range(N)]
    return np.stack([a for a, b in q]), np.stack([mx_ref.plane(b, rng) for a, b in q])
def values_of_codes():
    e, c = np.zeros((128, 128, 4), np.float32), np.zeros((128, 2, 4), np.uint8)
    e[np.arange(128), np.arange(128), 0] = 1
    c[:127, :, 0] = np.arange(256).reshape(2, 128).T[:127]
    return mx_ref.matmul(mx_ref.quantize(e.reshape(128, 512).astype(BF)), (c.reshape(128, 8), np.full((16, 2), 127, np.uint8))).T.reshape(-1).astype(np.float64)
CODE_VALUE, SCALE_VALUE = values_of_codes(), 2.0 ** (np.arange(256) - 127.0)
def decode(q):
    return (CODE_VALUE[q[0]].reshape(16, 8, -1, 4) * SCALE_VALUE[q[1]][:, None, :, None] + 0.0).reshape(128, -1).astype(np.float32)
def f(rng, *shape):
    return mx_ref.flush((rng.standard_normal(shape, dtype=np.float32) * np.exp2(rng.integers(-2, 3, shape[:-1] + (1,)))).astype(BF))
def wide(rng, *shape, cols=0):
    v = rng.standard_normal(shape, dtype=np.float32) * np.exp2(rng.integers(-12, 13, shape)).astype(np.float32)
    if cols: v *= np.repeat(np.exp2(rng.integers(-cols, cols + 1, shape[:-2] + (1, shape[-1] // 4))) * (rng.random(shape[:-2] + (1, shape[-1] // 4)) > 0.0625), 4, axis=-1).astype(np.float32)
    return mx_ref.flush(v.astype(BF))
C, L1, H1, L2, H2, K, R = 320, 128, 192, 80, 104, 112, 3
def big(v):
    v = v.astype(np.float32)
    v[np.abs(v) < np.float32(2.0 ** -16)] = 0
    return v.astype(BF)
def numbers_of(rng):
    return {"x": big(f(rng, N, 128, 4 * C)), "u": np.array(f(rng, N, 128, 512)), "v": np.array(f(rng, N, 128, 512))}
def layers(rng):
    return big(f(rng, N, 128, 2048)).reshape(N, 8, 16, 4, 8, 16, 4)
def weights(rng, w):
    c, p = packed(np.ascontiguousarray(w).reshape(N, 128, 2048), rng)
    return {"wc": c, "ws": p}
def setup_inputs(rng):
    return {**numbers_of(rng), **weights(rng, layers(rng))}
def setup_inputs_ties(rng):
    d = numbers_of(rng)
    x = d["x"].reshape(N, 8, 16, C, 4)
    x[:, :, 0] = 0
    x[:, :, 0, :, :2] = np.where(rng.random((N, 8, C, 2)) < 0.125, 3, rng.integers(1, 3, (N, 8, C, 2))).astype(np.float32).astype(BF)
    u = d["u"].reshape(N, 128, 128, 4)
    u[:, :, ::16] = 0
    u[:, :, 1::16] = 0
    e = int(rng.integers(N))
    k = rng.permutation(N - 2) % 2 * 2.0 - 1.0
    for i in range(N - 2):
        r = (e + 1 + i) % N
        for h in range(0, 128, 16):
            u[r, h, h, 0] = k[i]
            u[r, h, h + 1, 1] = k[i]
    w = layers(rng)
    w[:, :, :, :, :, 0] = 0
    return {"x": x.reshape(N, 128, 4 * C), "u": u.reshape(N, 128, 512), "v": d["v"], **weights(rng, w)}
def setup_inputs_near(rng):
    d = numbers_of(rng)
    x = d["x"].astype(np.float32).reshape(N, 8, 16, C, 4)
    x[:, :, 0] = 0
    x[:, :, 8:] = 0
    u = d["u"].reshape(N, 128, 128, 4)
    u[:, :, ::16] = 0
    u[:, :, 1::16] = 0
    o = rng.permutation(N) % 4
    for r in range(N):
        k = 1.0 if o[r] == 0 else 2.0 ** -30
        if o[r] < 3:
            s = rng.integers(0, 16, (8, C))
            x[r, :, 8] = ((s[:, :, None] >> np.arange(4)) & 1) * np.exp2(np.arange(4) - 23.0)
        if o[r] < 2:
            x[r, :, 0, :, 0] = 1.0 - 2.0 * o[r]
            x[r, :, 11, :, 0] = 2.0 ** -10
        if o[r] == 2: x[r, :, 0, :, 0] = -1.0 * (rng.random((8, C)) < 0.25)
        if o[r] == 3:
            s = rng.random((8, C)) < 0.25
            x[r, :, 10, :, 0] = np.where(s, 9.0, 0.0) * 2.0 ** -32
            x[r, :, 12, :, 0] = np.where(s, 0.0, 8.0) * 2.0 ** -32
        for h in range(0, 128, 16):
            for i in (h, h + 1):
                u[r, h, i, 0] = 1.0 if o[r] == 2 else k
                u[r, h + 8, i] = k
                u[r, h + 10, i, 0] = k * 1.125
                u[r, h + 11, i, 0] = k
                u[r, h + 12, i, 0] = k * 1.25
    w = layers(rng)
    w[:, :, :, :, :, 0] = 0
    w[:, :, :, :, :, 8:] = 0
    return {"x": x.reshape(N, 128, 4 * C).astype(BF), "u": u.reshape(N, 128, 512), "v": d["v"], **weights(rng, w)}
def setup_inputs_huge(rng):
    d = numbers_of(rng)
    e = rng.permutation(N)
    x = -0.6 - 0.4 * rng.random((N, 8, 16, C, 4))
    a = 0.9 + 0.1 * rng.random((N, 128, 128, 4))
    x[e[0], :, :15] = -1.0
    for i in (L1 - 1, H1 + 1): x[e[0], :, :, i] = -0.625
    a[e[0]] = 1.0
    u = d["u"].astype(np.float32).reshape(N, 128, 128, 4)
    for r in range(N):
        both = r in e[1::2]
        if both: x[r] *= rng.choice([-1.0, 1.0], (8, 1, C, 1))
        for h in range(0, 128, 16):
            i = slice(h, h + 16) if both else slice(0, 128)
            u[r, :, h:h + 2] = 0
            u[r, i, h:h + 2] = 2.0 ** 30 * a[r, i, h:h + 2]
    w = np.zeros((N, 128, 4, 128, 4), np.float32)
    i = np.arange(128)
    for b in range(4): w[:, i, b, i, b] = -1
    return {"x": (2.0 ** 30 * x).astype(np.float32).reshape(N, 128, 4 * C).astype(BF), "u": u.astype(BF).reshape(N, 128, 512), "v": d["v"], **weights(rng, w.astype(BF))}
def setup_inputs_edge(rng):
    d = numbers_of(rng)
    x = d["x"].reshape(N, 8, 16, C, 4)
    c = np.where(rng.random((N, 8)) < 0.25, rng.integers(L1, H1 + 1, (N, 8)), rng.choice([L1, H1], (N, 8)))
    k = np.where(rng.random((N, 8)) < 0.25, rng.integers(L2, H2 + 1, (N, 8)), rng.choice([L2, H2], (N, 8)))
    e = int(rng.integers(N))
    for r in (e, (e + 1) % N):
        c[r] = H1
        k[r] = L2
    x[:, :, 0] = 0
    x[:, :, 0, :, :2] = rng.integers(-1, 2, (N, 8, C, 2)).astype(np.float32).astype(BF)
    for i in (L1 - 1, H1 + 1): x[:, :, 0, i, 0] = 4.0
    for i in (L2 - 1, H2 + 1): x[:, :, 0, i, 1] = 4.0
    for r in range(N):
        for g in range(8):
            x[r, g, 0, c[r, g], 0] = 2.0
            x[r, g, 0, k[r, g], 1] = 2.0
    n = (N, 8, 8, C, 4)
    s = np.exp2(-1.0 * rng.integers(8, 15, n)) * (1.0 + (2 * rng.integers(0, 64, n) + 1) * 2.0 ** -7) * rng.choice([-1.0, 1.0], n)
    s[:, :, 0, :, 0] = 1.96875 * rng.choice([-1.0, 1.0], (N, 8, C))
    x[:, :, 8:] = s.astype(np.float32).astype(BF)
    u = d["u"].reshape(N, 128, 128, 4)
    u[:, :, ::16] = 0
    u[:, :, 1::16] = 0
    for h in range(0, 128, 16):
        u[:, h, h, 0] = 1
        u[:, h, h + 1, 1] = 1
    return {"x": x.reshape(N, 128, 4 * C), "u": u.reshape(N, 128, 512), "v": d["v"], **weights(rng, layers(rng))}
def setup_inputs_spread(rng):
    d = setup_inputs(rng)
    d["x"] = big(wide(rng, N, 128, 4 * C, cols=6))
    return d
def check_inputs(d):
    b = []
    for k in ("x", "u", "v"):
        a = np.abs(d[k].astype(np.float32))
        if not (np.isfinite(a).all() and ((a == 0) | (a >= 2.0 ** -30) & (a <= 2.0 ** 30)).all()): b.append("a value of " + k)
    none, least, most = [emit(mx_ref.quantize(np.full((128, 16), k, np.float32).astype(BF)))[1][0, 0] for k in (0.0, 2.0 ** -30, 2.0 ** 30)]
    for r in range(N):
        if ((d["wc"][r] == 0x7F) | (d["wc"][r] == 0xFF)).any(): b.append("wc: a code that is no number")
        s = mx_ref.live(d["ws"][r])
        if ((s != none) & ((s < least) | (s > most))).any(): b.append("ws: a scale out of range")
    return b
def folded(c, k):
    p = np.arange(C)
    q = np.where(p < c, c - 1 - p, p - c)
    z = np.where(q < k, k - 1 - q, q - k)
    right = (p >= c).astype(np.int64)
    leaf = np.where(q < k, right, 3 - right)
    o = np.argsort(4 * z + leaf, axis=1)
    zo = np.take_along_axis(z, o, axis=1)
    first = np.ones((8, C), bool)
    first[:, 1:] = zo[:, 1:] != zo[:, :-1]
    low, above = np.full((8, K), -1), C + z
    g, j = np.nonzero(first)
    low[g, zo[g, j]] = o[g, j]
    g, j = np.nonzero(~first)
    above[g, o[g, j - 1]] = o[g, j]
    return o, low, above
def reference(x, u, v, wc, ws):
    qu = [mx_ref.quantize(u[r]) for r in range(N)]
    lay = [pk(wc[r], ws[r]) for r in range(N)]
    now = [x[r] for r in range(N)]
    for t in range(R):
        own, folds, sent = [], [], []
        for r in range(N):
            q = mx_ref.quantize(now[r])
            own.append(decode(q))
            s = mx_ref.matmul(qu[r], q) + np.float32(0.0)
            c = L1 + np.argmax(s[::16, L1:H1 + 1], axis=1)
            k = L2 + np.argmax(s[1::16, L2:H2 + 1], axis=1)
            folds.append(folded(c[:, None], k[:, None]))
            sent.append(mx_ref.quantize(gcols(now[r], folds[r][1])))
        came = decode(join(*sent)).astype(BF)
        for r in range(N):
            o, low, above = folds[r]
            a = np.concatenate([own[r].astype(BF), cut(came, (r + 1) % N, 4 * K)], axis=1)
            z = mx_ref.quantize(((own[r] + gcols(a, above).astype(np.float32)) * np.float32(0.5)).astype(BF))
            made = tile([mx_ref.matmul(pick(lay[r], np.arange(128 * b, 128 * b + 128)), z) * np.float32(0.03125) + own[r][:, b::4] for b in range(4)])
            now[r] = gcols(made, o)
    y, lo = np.zeros((N, 128, C), np.float32), np.zeros((N, 8, C), np.float32)
    oc, osc = np.zeros((N, 128, 4 * C), np.uint8), np.zeros((N, 16, C), np.uint8)
    for r in range(N):
        q = mx_ref.quantize(now[r])
        y[r] = mx_ref.matmul(mx_ref.quantize(v[r]), q)
        lo[r] = folds[r][0]
        oc[r], osc[r] = emit(q)
    return {"y": y, "lo": lo, "oc": oc, "osc": osc}

@@ -1,0 +1,373 @@
+import numpy as np
+from concourse.mybir import AluOpType as Op, AxisListType, ActivationFunctionType as Fn, dt
+
+PAD = 256
+XW = 1280 + 2 * PAD
+FCOLS = [
+    ("R0", (0, 2, 0), (2, -2, 0)), ("B1", (2, 2, -320), (0, 0, 0)),
+    ("R1", (2, 2, -320), (-2, -2, 1320)), ("tau", (-1, -3, -319), (-2, 2, 640)),
+    ("m4", (-4, -4, 1280), (8, 0, -1280)), ("de", (1, -2, 0), (-2, 0, 320)),
+    ("d2", (-2, 4, 0), (4, 0, -640)), ("X", (0, 0, -1), (0, 0, 2)), ("Z", (-1, 0, 319.5), (0, 0, -319)),
+]
+NCOLS = [
+    ("ck", (1, -1, 0)), ("base", (1, -1, 319)), ("n2n", (1, 1, -320)), ("cpk", (1, 1, 0)), ("c", (1, 0, 0)),
+    ("cm", (1, 0, -0.5)), ("X1", (-1, 1, 320)), ("k2n", (0, -2, 0)), ("k2", (0, 2, 0)), ("kh", (0, -1, 0.5)),
+]
+NF, NN = len(FCOLS), len(NCOLS)
+NL = 2 * NF + NN
+LIN = [a for _, a, _ in FCOLS] + [a for _, a in NCOLS] + [b for _, _, b in FCOLS]
+SCOL = {n: i for i, n in enumerate([n for n, _, _ in FCOLS] + [n for n, _ in NCOLS])}
+
+F8, U8, BF, F32, I32, U16 = "float8_e4m3fn_x4", "uint8", "bfloat16", "float32", "int32", "uint16"
+SCRATCH = {"PS": ("psum", [128, 4096], F32)}
+for _n, _w in (("X0", XW), ("X1", XW), ("X2", XW), ("X3", 1280), ("UT", 512), ("VT", 512), ("BT", 512), ("ZT", 1280), ("PL", 1728),
+               ("FP", 640), ("AB", 640), ("YP", 1280), ("ED", 516), ("EDB", 516), ("HALF", 516)):
+    SCRATCH[_n] = ("sbuf", [128, _w], BF)
+for _n, _w in (("QU", 128), ("UU", 256), ("QV", 128), ("QW", 512), ("EH", 512), ("EB", 512), ("QS", 128), ("QX", 320), ("QZ", 320),
+               ("QF", 320), ("QN", 128), ("B0", 128), ("B1", 128), ("B2", 128), ("G0", 128), ("G1", 128), ("G2", 128)):
+    SCRATCH[_n] = ("sbuf", [128, _w], F8)
+    SCRATCH[_n + "s"] = ("sbuf", [128, _w], U8)
+for _n, _w in (("C16", 28), ("TJB", 28), ("TP", 20), ("TN", 20), ("Z4", 8), ("CZ", 8), ("LANE", 5), ("JF", 76), ("EP", 76), ("NIL", 68),
+               ("AL", NL), ("BE", NL), ("GA", NL), ("IOT", 320), ("LOR", 320), ("YO", 320), ("RMC", 65), ("RMK", 25), ("LTC", 66), ("LTK", 26),
+               ("CK", 2), ("S1", NL), ("S2", NL), ("S3", NL), ("S4", NL), ("FS", NF), ("FV", NF), ("SM", 16), ("W2", 64), ("WA", 320), ("WO", 1024), ("EI", 76), ("EJ", 76)):
+    SCRATCH[_n] = ("sbuf", [128, _w], F32)
+for _n, _w in (("LI", 5), ("JI", 76), ("IA", 76), ("IB", 76), ("IC", 76), ("PO", 16), ("OQ", 56), ("OS", 56), ("O0", 56), ("O1", 56), ("OZ", 56)):
+    SCRATCH[_n] = ("sbuf", [128, _w], I32)
+for _n, _w in (("PU", 16), ("L1", 20), ("L2", 8), ("LA", 20), ("LO", 56)):
+    SCRATCH[_n] = ("sbuf", [128, _w], U16)
+SEMAPHORES = ["v", "a", "te", "gc", "dx", "du", "dv", "dw", "dn", "out", "arr0", "arr1", "arr2", "sent"]
+
+
+def rank_program(g, core, T, topo):
+    rank = T.rank_of(core)
+    if rank is None:
+        return
+    N = len(T.cores)
+    prev, nxt = T.cores[(rank - 1) % N], T.cores[(rank + 1) % N]
+    queue = {"v": g.vector, "a": g.scalar, "te": g.tensor, "gc": g, "sy": g.sync}
+    total, known = {}, {}
+
+    def wait(q, deps):
+        need = {}
+        for s, n in deps:
+            need[s] = max(need.get(s, 0), n)
+        for s, n in need.items():
+            if known.get((q, s), 0) < n:
+                queue[q].wait_ge(T.sem[s], n)
+                known[(q, s)] = n
+
+    def run(q, fn, deps=()):
+        wait(q, deps)
+        ins = fn(queue[q])
+        total[q] = total.get(q, 0) + 1
+        ins.then_inc(T.sem[q], 1)
+        return (q, total[q])
+
+    def dma(q, out, in_, sem, deps=()):
+        wait(q, deps)
+        queue[q].dma_start(out, in_).then_inc(T.sem[sem], 16)
+        total[sem] = total.get(sem, 0) + 16
+        return (sem, total[sem])
+
+    def ts(out, in0, s1, op0, s2=None, op1=None, deps=()):
+        if op1 is None:
+            return run("v", lambda q: q.tensor_scalar(out, in0, s1, None, op0), deps)
+        return run("v", lambda q: q.tensor_scalar(out, in0, s1, s2, op0, op1), deps)
+
+    def tt(out, a, b, op, deps=()):
+        return run("v", lambda q: q.tensor_tensor(out, a, b, op), deps)
+
+    def vcopy(out, in_, deps=()):
+        return run("v", lambda q: q.tensor_copy(out, in_), deps)
+
+    def acopy(out, in_, deps=(), scale=1.0):
+        return run("a", lambda q: q.activation(out, in_, Fn.Copy, scale=scale), deps)
+
+    def quant(name, lo, hi, in_, deps=()):
+        return run("v", lambda q: q.quantize_mx(T[name][:, lo:hi], T[name + "s"][:, lo:hi], in_), deps)
+
+    def mm(bank, n, w, wlo, x, xlo, deps=(), start=True, stop=True):
+        return run("te", lambda q: q.matmul_mx(T.PS[:, 512 * bank:512 * bank + n], T[w][:, wlo:wlo + 128], T[w + "s"][:, wlo:wlo + 128],
+                                               T[x][:, xlo:xlo + n], T[x + "s"][:, xlo:xlo + n], start, stop), deps)
+
+    def bank(b, lo, hi):
+        return T.PS[:, 512 * b + lo:512 * b + hi]
+
+    def fill(ap, value):
+        return run("v", lambda q: q.memset(ap, value))
+
+    def iota(ap, pattern, base, cm, flag=True):
+        if flag:
+            return run("gc", lambda q: q.iota(ap, pattern, base, cm, allow_small_or_imprecise_dtypes=True))
+        return run("gc", lambda q: q.iota(ap, pattern, base, cm))
+
+    dx = dma("sy", T.X0[:, PAD:PAD + 1280], T.x[:], "dx")
+    du = dma("a", T.UT[:], T.u[:], "du")
+    dma("sy", T.QW[:].bitcast(dt.uint8), T.wc[:], "dw")
+    dw = dma("sy", T.QWs[:], T.ws[:], "dw")
+    dv = dma("sy", T.VT[:], T.v[:], "dv")
+
+    t_half = fill(T.HALF[:], 0.5)
+    t_nil = fill(T.NIL[:], 0.0)
+    t_bt = fill(T.BT[:], 0.0)
+    fill(T.LTC[:, 65:66], 512.0)
+    t_lt = fill(T.LTK[:, 25:26], 320.0)
+    t_po = iota(T.PO[:], [[1, 2], [16, 8]], 0, 0, flag=False)
+    t_li = iota(T.LI[:, 0:1], [[0, 1]], 0, 1, flag=False)
+    t_c16 = iota(T.C16[:], [[16, 28]], 0, 0)
+    for o in (0, PAD + 1280):
+        t_pad0 = iota(T.X0[:, o:o + PAD], [[0, PAD]], 0, 0)
+    t_ed = run("gc", lambda q: q.affine_select(T.ED[:], T.HALF[:], [[-1, 516]], Op.is_equal, 0.0, 3, 4), [t_half])
+    iota(T.JF[:, 0:8], [[16, 8]], 80, 0)
+    iota(T.JF[:, 8:28], [[4, 20]], 0, 0)
+    iota(T.JF[:, 28:56], [[4, 28]], 208, 0)
+    t_jf = iota(T.JF[:, 56:76], [[16, 20]], 0, 0)
+    for n in ("X1", "X2"):
+        for o in (0, PAD + 1280):
+            t_pad = iota(T[n][:, o:o + PAD], [[0, PAD]], 0, 0)
+    t_iot = iota(T.IOT[:], [[1, 320]], 0, 0)
+    t_pu = vcopy(T.PU[:], T.PO[:], [t_po])
+    ts(T.LI[:, 1:2], T.LI[:, 0:1], 15, Op.bitwise_and, deps=[t_li])
+    ts(T.LI[:, 2:3], T.LI[:, 0:1], 12, Op.bitwise_and)
+    ts(T.LI[:, 3:4], T.LI[:, 0:1], 12, Op.bitwise_and)
+    t_l3 = ts(T.LI[:, 4:5], T.LI[:, 0:1], 3, Op.bitwise_and)
+    t_lane = vcopy(T.LANE[:], T.LI[:], [t_l3])
+    t_l = [t_lane,
+           ts(T.LANE[:, 3:4], T.LANE[:, 2:3], 0.25, Op.mult, deps=[t_lane]),
+           ts(T.LANE[:, 4:5], T.LANE[:, 4:5], 320.0, Op.mult)]
+    lane, l4, l1, b320 = (T.LANE[:, i:i + 1] for i in (1, 2, 3, 4))
+    t_tjb = ts(T.TJB[:], T.C16[:], lane, Op.add, float(PAD), Op.add, [t_c16] + t_l)
+    ts(T.Z4[:], T.C16[:, 20:28], l4, Op.add)
+    t_cz = ts(T.CZ[:], T.C16[:, 20:28], l4, Op.add, 2.0, Op.add)
+    t_qu = quant("QU", 0, 128, T.UT[:], [du])
+    t_uc = run("v", lambda q: q.tensor_copy(T.UU[:].bitcast(dt.uint32), T.QU[:].bitcast(dt.uint32).indirect(T.PU[:])), [t_qu, t_pu])
+    t_us = run("a", lambda q: q.activation(T.UUs[:], T.QUs[:].indirect(T.PU[:]), Fn.Copy), [t_qu, t_pu])
+    t_qn = quant("QN", 0, 128, T.BT[:], [t_bt])
+    for t in range(3):
+        dma("sy", T["G%d" % t][:, 112:128].bitcast(dt.uint8), T.QN[:, 112:128].bitcast(dt.uint8), "dn", [t_qn])
+        t_gn = dma("sy", T["G%ds" % t][:, 112:128], T.QNs[:, 112:128], "dn")
+
+    def coefficients(put, name, i):
+        j = 0
+        while j < NL:
+            e = j
+            while e < NL and LIN[e][i] == LIN[j][i]:
+                e += 1
+            tok = put(T[name][:, j:e], float(LIN[j][i]), e - j)
+            j = e
+        return tok
+
+    def by_scalar(ap, value, n):
+        return run("a", lambda q: q.activation(ap, T.NIL[:, 0:n], Fn.Identity, bias=value), [t_nil])
+
+    t_be = coefficients(by_scalar, "BE", 1)
+    t_ga = coefficients(by_scalar, "GA", 2)
+    t_edb = acopy(T.EDB[:], T.ED[:], [t_ed], scale=64.0)
+
+    def later_constants():
+        ta = coefficients(lambda ap, value, n: fill(ap, value), "AL", 0)
+        for b in range(4):
+            te = quant("EB", 128 * b, 128 * b + 128, T.EDB[:, 3 - b:515 - b], [t_edb])
+        ts(T.TP[:], T.C16[:, 0:20], lane, Op.add)
+        t1 = ts(T.JF[:, 0:8], T.JF[:, 0:8], lane, Op.add, deps=[t_jf])
+        t2 = ts(T.JF[:, 8:56], T.JF[:, 8:56], l1, Op.add)
+        t3 = ts(T.JF[:, 56:76], T.JF[:, 56:76], lane, Op.add)
+        ts(T.TN[:], T.TP[:], -1.0, Op.mult, deps=[t1])
+        vcopy(T.JI[:], T.JF[:], [t3])
+        t4 = ts(T.IA[:], T.JF[:], -1.0, Op.mult, 319.0, Op.add)
+        t5 = ts(T.IB[:], T.IA[:], 1, Op.bitwise_and, deps=[t4])
+        t6 = ts(T.IC[:], T.IA[:], 1, Op.logical_shift_right)
+        t7 = ts(T.EI[:], T.IB[:], -2.0, Op.mult, 1.0, Op.add, deps=[t5])
+        t8 = ts(T.EJ[:], T.IC[:], 0.5, Op.add, deps=[t6])
+        t9 = tt(T.EP[:], T.EI[:], T.EJ[:], Op.mult, deps=[t7, t8])
+        return [ta, t9, t_be, t_ga], te
+
+    for b in range(4):
+        t_eh = quant("EH", 128 * b, 128 * b + 128, T.ED[:, 3 - b:515 - b], [t_ed])
+
+    CK, FV, SMT, WA, WO = T.CK, T.FV, T.SM, T.WA, T.WO
+    C4, K4 = CK[:, 0:1], CK[:, 1:2]
+
+    def sc(name):
+        i = SCOL[name]
+        return FV[:, i:i + 1] if i < NF else T.S4[:, i:i + 1]
+
+    def lists(last, t_ck, t_const):
+        o = (56, 76) if last else (0, 56)
+        w = o[1] - o[0]
+        J, JI, E, P = T.JF[:, o[0]:o[1]], T.JI[:, o[0]:o[1]], T.EP[:, o[0]:o[1]], T.TP[:]
+        wa = lambda i: WA[:, 20 * i:20 * i + 20]
+        wo = lambda i: WO[:, 64 * i:64 * i + w]
+        it = lambda n: T[n][:, 0:w]
+        k = {"ck": t_ck, "con": t_const}
+
+        def step(name, fn, *deps):
+            k[name] = fn([x for d in deps for x in (k[d] if isinstance(k[d], list) else [k[d]])])
+
+        fv = SMT[:, 0:1]
+        step("f", lambda d: ts(fv, C4, 640.0, Op.is_lt, deps=d), "ck")
+        step("s1", lambda d: ts(T.S1[:], T.AL[:], C4, Op.mult, 0.25, Op.mult, d), "ck", "con")
+        step("s2", lambda d: ts(T.S2[:], T.BE[:], K4, Op.mult, 0.25, Op.mult, d), "ck", "con")
+        step("s3", lambda d: tt(T.S3[:], T.S1[:], T.GA[:], Op.add, d), "s1")
+        step("s4", lambda d: tt(T.S4[:], T.S3[:], T.S2[:], Op.add, d), "s3", "s2")
+        step("fs", lambda d: ts(T.FS[:], T.S4[:, NF + NN:NL], fv, Op.mult, deps=d), "s4", "f")
+        ops_a = [
+            ("m1", lambda d: ts(wa(0), P, sc("ck"), Op.is_ge, sc("n2n"), Op.mult, d), "s4"),
+            ("m2", lambda d: ts(wa(1), P, sc("c"), Op.is_ge, sc("X1"), Op.mult, d), "s4"),
+            ("m4x", lambda d: ts(wa(3), P, sc("cpk"), Op.is_ge, sc("k2n"), Op.mult, d), "s4"),
+            ("a1", lambda d: tt(wa(8), wa(0), T.TN[:], Op.add, d), "m1"),
+            ("RB", lambda d: ts(SMT[:, 2:4], FV[:, 0:2], sc("c"), Op.max, deps=d), "fv"),
+            ("r2", lambda d: ts(wa(5), P, sc("R1"), Op.is_lt, deps=d), "fv"),
+            ("w", lambda d: ts(wa(6), P, 2.0, Op.mult, sc("tau"), Op.add, d), "fv"),
+            ("m3", lambda d: ts(wa(2), P, SMT[:, 3:4], Op.is_ge, sc("n2n"), Op.mult, d), "RB"),
+            ("r1", lambda d: ts(wa(4), P, SMT[:, 2:3], Op.is_ge, deps=d), "RB"),
+            ("rw", lambda d: tt(wa(7), wa(5), wa(6), Op.mult, d), "r2", "w"),
+            ("a2", lambda d: tt(wa(9), wa(1), wa(2), Op.add, d), "m2", "m3"),
+            ("rv", lambda d: tt(wa(10), wa(4), wa(7), Op.mult, d), "r1", "rw"),
+            ("a4", lambda d: tt(wa(11), wa(8), wa(9), Op.add, d), "a1", "a2"),
+            ("a3", lambda d: tt(wa(12), wa(10), wa(3), Op.add, d), "rv", "m4x"),
+            ("a5", lambda d: tt(wa(13), wa(11), wa(12), Op.add, d), "a4", "a3"),
+            ("LA", lambda d: ts(T.LA[:], wa(13), sc("base"), Op.add, deps=d), "a5"),
+        ]
+        ops_o = [
+            ("fv", lambda d: tt(FV[:], T.FS[:], T.S4[:, 0:NF], Op.add, d), "fs"),
+            ("t", lambda d: ts(wo(0), J, sc("m4"), Op.subtract, 0.0, Op.max, d), "fv"),
+            ("mx", lambda d: tt(SMT[:, 4:5], sc("de"), sc("d2"), Op.max, d), "fv"),
+            ("Q", lambda d: ts(it("OQ"), wo(0), fv, Op.subtract, 1.0 / 3.0, Op.mult, d), "t"),
+            ("ge", lambda d: ts(SMT[:, 5:6], sc("de"), 0.0, Op.is_ge, deps=d), "fv"),
+            ("s", lambda d: tt(it("OS"), it("OQ"), JI, Op.add, d), "Q"),
+            ("hm", lambda d: ts(SMT[:, 6:7], sc("de"), 0.0, Op.is_lt, deps=d), "fv"),
+            ("b1", lambda d: ts(it("O1"), it("OS"), 1, Op.logical_shift_right, 1, Op.bitwise_and, d), "s"),
+            ("z", lambda d: ts(it("OZ"), it("OS"), 2, Op.logical_shift_right, deps=d), "s"),
+            ("b0", lambda d: ts(it("O0"), it("OS"), 1, Op.bitwise_and, deps=d), "s"),
+            ("sk", lambda d: ts(wo(1), it("O1"), sc("k2"), Op.mult, sc("kh"), Op.add, d), "b1"),
+            ("gxz", lambda d: ts(SMT[:, 8:10], FV[:, SCOL["X"]:SCOL["Z"] + 1], SMT[:, 5:6], Op.mult, deps=d), "ge"),
+            ("s12", lambda d: ts(wo(2), it("O0"), -2.0, Op.mult, 1.0, Op.add, d), "b0"),
+            ("u", lambda d: tt(wo(3), wo(1), it("OZ"), Op.add, d), "sk", "z"),
+            ("e1", lambda d: ts(wo(4), J, SMT[:, 8:9], Op.mult, SMT[:, 9:10], Op.add, d), "gxz"),
+            ("e2", lambda d: ts(wo(5), E, SMT[:, 6:7], Op.mult, deps=d), "hm"),
+            ("p12", lambda d: tt(wo(6), wo(2), wo(3), Op.mult, d), "s12", "u"),
+            ("p3", lambda d: tt(wo(7), wo(4), wo(5), Op.add, d), "e1", "e2"),
+            ("mk", lambda d: ts(wo(8), J, SMT[:, 4:5], Op.add, 320.0, Op.is_ge, d), "mx"),
+            ("df", lambda d: tt(wo(9), wo(7), wo(6), Op.subtract, d), "p3", "p12"),
+            ("dm", lambda d: tt(wo(10), wo(9), wo(8), Op.mult, d), "df", "mk"),
+            ("pl", lambda d: tt(wo(11), wo(10), wo(6), Op.add, d), "dm"),
+        ]
+        if last:
+            ops_o.append(("LO", lambda d: ts(T.LO[:, 0:20], wo(11), sc("cm"), Op.add, deps=d), "pl"))
+        else:
+            ops_o.append(("LOx", lambda d: ts(T.LO[:, 0:8], WO[:, 704:712], sc("cm"), Op.add, deps=d), "pl"))
+            ops_o.append(("LO", lambda d: ts(T.LO[:, 8:56], WO[:, 712:760], sc("cm"), Op.add, b320, Op.add, d), "pl"))
+        na, no = len(ops_a), len(ops_o)
+        i = 0
+        for j in range(no):
+            step(*ops_o[j])
+            while i < na and (i + 1) * no <= (j + 1) * na:
+                step(*ops_a[i])
+                i += 1
+        return k["LA"], k["LO"]
+
+    first, rest = [dx], [dx, t_pad0]
+    for t in range(3):
+        X, last = T["X%d" % t], t == 2
+        t_qs = quant("QS", 0, 128, X[:, PAD + 320:PAD + 832], first)
+        if t == 0:
+            t_s1 = mm(6, 128, "UU", 0, "QS", 0, [t_qs, t_uc, t_us])
+        else:
+            t_s1 = mm(6, 128, "UU", 0, "QS", 0, [t_qs])
+        t_s2 = mm(7, 128, "UU", 128, "QS", 0)
+        t1 = run("v", lambda q: q.tensor_tensor_scan(T.RMC[:], T.NIL[:, 0:65], bank(6, 48, 113), -1e29, Op.add, Op.max), [t_s1, t_nil])
+        t2 = run("v", lambda q: q.tensor_tensor_scan(T.RMK[:], T.NIL[:, 0:25], bank(7, 0, 25), -1e29, Op.add, Op.max), [t_s2])
+        t3 = ts(T.LTC[:, 0:65], T.RMC[:], T.RMC[:, 64:65], Op.is_lt, 4.0, Op.mult, [t1])
+        t4 = ts(T.LTK[:, 0:25], T.RMK[:], T.RMK[:, 24:25], Op.is_lt, 4.0, Op.mult, [t2])
+        t5 = run("v", lambda q: q.tensor_reduce(C4, T.LTC[:], AxisListType.X, Op.add), [t3, t_lt])
+        t6 = run("v", lambda q: q.tensor_reduce(K4, T.LTK[:], AxisListType.X, Op.add), [t4])
+        t_l1 = ts(T.L1[:], T.TJB[:, 0:20], C4, Op.add, K4, Op.subtract, [t5, t6, t_tjb])
+        t_b1 = acopy(T.BT[:, 0:320], X[:].indirect(T.L1[:]), [t_l1, t_qn] + rest)
+        w2 = lambda i: T.W2[:, 8 * i:8 * i + 8]
+        fm, kf = T.SM[:, 12:13], T.SM[:, 13:14]
+        t7 = ts(fm, C4, 640.0, Op.is_ge, -1.0, Op.mult)
+        t8 = ts(w2(0), T.Z4[:], K4, Op.is_ge, 2.0, Op.mult, [t_cz])
+        t9 = ts(kf, fm, 1.0, Op.add, K4, Op.mult, [t7])
+        t10 = ts(w2(1), T.CZ[:], fm, Op.mult, kf, Op.add, [t9])
+        t11 = tt(w2(2), w2(0), w2(1), Op.mult, [t8, t10])
+        t12 = tt(w2(3), w2(2), T.TJB[:, 20:28], Op.add, [t11])
+        t_l2 = ts(T.L2[:], w2(3), C4, Op.add, K4, Op.subtract, [t12])
+        t_b2 = vcopy(T.BT[:, 320:448], X[:].indirect(T.L2[:]), [t_l2] + rest)
+        B, G = "B%d" % t, "G%d" % t
+        t_qb = quant(B, 0, 128, T.BT[:], [t_b1, t_b2])
+        engines = topo.engines(core, prev)[:8]
+        mask = sum(1 << e for e in engines)
+        rid, pid = topo.addr(prev)[:2]
+        wait("gc", [t_qb])
+        for out, in_ in ((T[G][:, 0:112].bitcast(dt.uint8), T[B][:, 0:112].bitcast(dt.uint8)), (T[G + "s"][:, 0:112], T[B + "s"][:, 0:112])):
+            g.remote_dma(out, in_, T.sem["arr%d" % t], T.sem.sent, pid, rid, mask)
+            total["sent"] = total.get("sent", 0) + len(engines)
+        total["arr%d" % t] = 2 * len(topo.engines(nxt, core)[:8])
+        t_qx = quant("QX", 0, 320, X[:, PAD:PAD + 1280], rest)
+        if t == 0:
+            t_con, t_eb = later_constants()
+        for b in range(4):
+            t_hf = mm(b, 320, "EH", 128 * b, "QX", 0, [t_qx, t_eh])
+            t_f = acopy(T.PL[:, 432 * b:432 * b + 320], bank(b, 0, 320), [t_hf])
+            if b < 2:
+                t_pl = acopy(T.FP[:, 320 * b:320 * b + 320], bank(b, 0, 320))
+        for b in range(2):
+            mm(b, 320, "EB", 128 * b, "QX", 0, [t_pl, t_eb], stop=False)
+        t_la, t_lo = lists(last, [t5, t6], t_con)
+        if t == 0:
+            t_qv = quant("QV", 0, 128, T.VT[:], [dv])
+        if last:
+            t_lor = run("a", lambda q: q.activation(T.LOR[:], T.IOT[:].indirect(T.LO[:, 0:20]), Fn.Copy), [t_lo, t_iot])
+            dma("sy", T.lo[:], T.LOR[0:128:16, :], "out", [t_lor])
+        arr = [("arr%d" % t, total["arr%d" % t]), t_gn]
+        t_g0 = mm(4, 128, "EH", 0, G, 0, arr)
+        t_g2 = mm(5, 128, "EH", 256, G, 0)
+        t_g1 = mm(6, 128, "EH", 128, G, 0)
+        t_g3 = mm(7, 128, "EH", 384, G, 0)
+        win = lambda b: T.PL[:, 432 * b:432 * b + 432]
+        t_c0 = vcopy(T.PL[:, 320:432], bank(4, 0, 112), [t_g0])
+        t_c2 = acopy(T.PL[:, 1184:1296], bank(5, 0, 112), [t_g2])
+        t_c1 = vcopy(T.PL[:, 752:864], bank(6, 0, 112), [t_g1])
+        t_a2 = acopy(T.AB[:, 0:320], win(2).indirect(T.LA[:]), [t_la, t_c2])
+        t_c3 = acopy(T.PL[:, 1616:1728], bank(7, 0, 112), [t_g3])
+        t_a3 = acopy(T.AB[:, 320:640], win(3).indirect(T.LA[:]), [t_c3])
+        mm(4, 320, "EB", 256, "QX", 0, [t_c0], stop=False)
+        mm(5, 320, "EB", 384, "QX", 0, [t_c2], stop=False)
+        tt(T.ZT[:, 0:1280:4], win(0).indirect(T.LA[:]), T.FP[:, 0:320], Op.add, [t_c0, t_f, t_la])
+        tt(T.ZT[:, 1:1280:4], win(1).indirect(T.LA[:]), T.FP[:, 320:640], Op.add, [t_c1])
+        tt(T.ZT[:, 2:1280:4], bank(2, 0, 320), T.AB[:, 0:320], Op.add, [t_a2])
+        t_z = tt(T.ZT[:, 3:1280:4], bank(3, 0, 320), T.AB[:, 320:640], Op.add, [t_a3])
+        t_qz = quant("QZ", 0, 320, T.ZT[:], [t_z])
+        t_r = [mm((0, 1, 4, 5)[b], 320, "QW", 128 * b, "QZ", 0, [t_qz, dw], start=False) for b in range(4)]
+        XN = T["X%d" % (t + 1)]
+        new = []
+        for b in range(4):
+            src, yp = bank((0, 1, 4, 5)[b], 0, 320), T.YP[:, 320 * b:320 * b + 320]
+            if b % 2 == 0:
+                ty = ts(yp, src, 0.03125, Op.mult, deps=[t_r[b]])
+            else:
+                ty = acopy(yp, src, [t_r[b]], scale=0.03125)
+            new.append(ty)
+            copy = vcopy if b % 2 == 0 else acopy
+            if last:
+                new.append(copy(XN[:, b:1280:4], yp.indirect(T.LO[:, 0:20]), [ty, t_lo]))
+            else:
+                new.append(copy(XN[:, PAD + 320 + b:PAD + 832:4], yp.indirect(T.LO[:, 0:8]), [ty, t_lo]))
+        first = list(new)
+        if not last:
+            r1 = acopy(XN[:, PAD:PAD + 320], T.YP[:].indirect(T.LO[:, 8:28]), new)
+            r2 = acopy(XN[:, PAD + 832:PAD + 1280], T.YP[:].indirect(T.LO[:, 28:56]))
+            rest = new + [r1, r2, t_pad]
+
+    t_qf = quant("QF", 0, 320, T.X3[:], first)
+    t_y0 = mm(2, 160, "QV", 0, "QF", 0, [t_qf, t_qv])
+    t_y1 = mm(3, 160, "QV", 0, "QF", 160)
+    dma("sy", T.oc[:], T.QF[:].bitcast(dt.uint8), "out", [t_qf])
+    t_o0 = vcopy(T.YO[:, 0:160], bank(2, 0, 160), [t_y0])
+    t_o1 = acopy(T.YO[:, 160:320], bank(3, 0, 160), [t_y1])
+    for k in range(4):
+        dma("sy" if k < 2 else "a", T.osc[4 * k:4 * k + 4, :], T.QFs[32 * k:32 * k + 4, :], "out", [t_qf])
+    dma("sy", T.y[:, 0:160], T.YO[:, 0:160], "out", [t_o0])
+    dma("a", T.y[:, 160:320], T.YO[:, 160:320], "out", [t_o1])
+    wait("gc", list(total.items()))

@@ -24,18 +24,19 @@ for _n, _w in (("X0", XW), ("X1", XW), ("X2", XW), ("X3", 1280), ("UT", 512), ("
                ("FP", 640), ("AB", 640), ("YP", 1280), ("ED", 516), ("EDB", 516), ("HALF", 516)):
     SCRATCH[_n] = ("sbuf", [128, _w], BF)
 for _n, _w in (("QU", 128), ("UU", 256), ("QV", 128), ("QW", 512), ("EH", 512), ("EB", 512), ("QS", 128), ("QX", 320), ("QZ", 320),
-               ("QF", 320), ("QN", 128), ("B0", 128), ("B1", 128), ("B2", 128), ("G0", 128), ("G1", 128), ("G2", 128)):
+               ("QF", 320), ("B0", 128), ("B1", 128), ("B2", 128), ("G0", 128), ("G1", 128), ("G2", 128)):
     SCRATCH[_n] = ("sbuf", [128, _w], F8)
     SCRATCH[_n + "s"] = ("sbuf", [128, _w], U8)
-for _n, _w in (("C16", 28), ("TJB", 28), ("TP", 20), ("TN", 20), ("Z4", 8), ("CZ", 8), ("LANE", 5), ("JF", 76), ("EP", 76), ("NIL", 68),
+for _n, _w in (("C16", 28), ("TJB", 28), ("TP", 20), ("TN", 20), ("Z4", 8), ("CZ", 8), ("LANE", 7), ("LAN2", 4), ("JF", 76), ("EP", 76), ("NIL", 68),
                ("AL", NL), ("BE", NL), ("GA", NL), ("IOT", 320), ("LOR", 320), ("YO", 320), ("RMC", 65), ("RMK", 25), ("LTC", 66), ("LTK", 26),
-               ("CK", 2), ("S1", NL), ("S2", NL), ("S3", NL), ("S4", NL), ("FS", NF), ("FV", NF), ("SM", 16), ("W2", 64), ("WA", 320), ("WO", 1024), ("EI", 76), ("EJ", 76)):
+               ("CK", 2), ("S1", NL), ("S2", NL), ("S3", NL), ("S4", NL), ("FS", NF), ("FV", NF), ("SM", 16), ("W2", 64), ("WA", 320), ("WO", 1024)):
     SCRATCH[_n] = ("sbuf", [128, _w], F32)
-for _n, _w in (("LI", 5), ("JI", 76), ("IA", 76), ("IB", 76), ("IC", 76), ("PO", 16), ("OQ", 56), ("OS", 56), ("O0", 56), ("O1", 56), ("OZ", 56)):
+for _n, _w in (("LI", 7), ("JI", 76), ("PO", 16), ("OQ", 56), ("OS", 56), ("O0", 56), ("O1", 56), ("OZ", 56)):
     SCRATCH[_n] = ("sbuf", [128, _w], I32)
 for _n, _w in (("PU", 16), ("L1", 20), ("L2", 8), ("LA", 20), ("LO", 56)):
     SCRATCH[_n] = ("sbuf", [128, _w], U16)
 SEMAPHORES = ["v", "a", "te", "gc", "dx", "du", "dv", "dw", "dn", "out", "arr0", "arr1", "arr2", "sent"]
+RBANK = ((0, 1, 4, 5), (6, 7, 2, 3))
 
 
 def rank_program(g, core, T, topo):
@@ -83,6 +84,9 @@ def rank_program(g, core, T, topo):
     def acopy(out, in_, deps=(), scale=1.0):
         return run("a", lambda q: q.activation(out, in_, Fn.Copy, scale=scale), deps)
 
+    def affine(out, in_, bias, scale=1.0, deps=()):
+        return run("a", lambda q: q.activation(out, in_, Fn.Identity, bias=bias, scale=scale), deps)
+
     def quant(name, lo, hi, in_, deps=()):
         return run("v", lambda q: q.quantize_mx(T[name][:, lo:hi], T[name + "s"][:, lo:hi], in_), deps)
 
@@ -107,148 +111,137 @@ def rank_program(g, core, T, topo):
     dw = dma("sy", T.QWs[:], T.ws[:], "dw")
     dv = dma("sy", T.VT[:], T.v[:], "dv")
 
-    t_half = fill(T.HALF[:], 0.5)
-    t_nil = fill(T.NIL[:], 0.0)
-    t_bt = fill(T.BT[:], 0.0)
-    fill(T.LTC[:, 65:66], 512.0)
-    t_lt = fill(T.LTK[:, 25:26], 320.0)
     t_po = iota(T.PO[:], [[1, 2], [16, 8]], 0, 0, flag=False)
     t_li = iota(T.LI[:, 0:1], [[0, 1]], 0, 1, flag=False)
     t_c16 = iota(T.C16[:], [[16, 28]], 0, 0)
+    fill(T.NIL[:], 0.0)
+    fill(T.AL[:], 0.0)
+    fill(T.BE[:], 0.0)
+    t_nil = fill(T.GA[:], 0.0)
+    t_half = fill(T.HALF[:], 0.5)
+    t_ed = run("gc", lambda q: q.affine_select(T.ED[:], T.HALF[:], [[-1, 516]], Op.is_equal, 0.0, 3, 4), [t_half])
     for o in (0, PAD + 1280):
         t_pad0 = iota(T.X0[:, o:o + PAD], [[0, PAD]], 0, 0)
-    t_ed = run("gc", lambda q: q.affine_select(T.ED[:], T.HALF[:], [[-1, 516]], Op.is_equal, 0.0, 3, 4), [t_half])
     iota(T.JF[:, 0:8], [[16, 8]], 80, 0)
     iota(T.JF[:, 8:28], [[4, 20]], 0, 0)
     iota(T.JF[:, 28:56], [[4, 28]], 208, 0)
     t_jf = iota(T.JF[:, 56:76], [[16, 20]], 0, 0)
-    for n in ("X1", "X2"):
-        for o in (0, PAD + 1280):
-            t_pad = iota(T[n][:, o:o + PAD], [[0, PAD]], 0, 0)
-    t_iot = iota(T.IOT[:], [[1, 320]], 0, 0)
-    t_pu = vcopy(T.PU[:], T.PO[:], [t_po])
-    ts(T.LI[:, 1:2], T.LI[:, 0:1], 15, Op.bitwise_and, deps=[t_li])
-    ts(T.LI[:, 2:3], T.LI[:, 0:1], 12, Op.bitwise_and)
-    ts(T.LI[:, 3:4], T.LI[:, 0:1], 12, Op.bitwise_and)
-    t_l3 = ts(T.LI[:, 4:5], T.LI[:, 0:1], 3, Op.bitwise_and)
-    t_lane = vcopy(T.LANE[:], T.LI[:], [t_l3])
-    t_l = [t_lane,
-           ts(T.LANE[:, 3:4], T.LANE[:, 2:3], 0.25, Op.mult, deps=[t_lane]),
-           ts(T.LANE[:, 4:5], T.LANE[:, 4:5], 320.0, Op.mult)]
-    lane, l4, l1, b320 = (T.LANE[:, i:i + 1] for i in (1, 2, 3, 4))
-    t_tjb = ts(T.TJB[:], T.C16[:], lane, Op.add, float(PAD), Op.add, [t_c16] + t_l)
-    ts(T.Z4[:], T.C16[:, 20:28], l4, Op.add)
-    t_cz = ts(T.CZ[:], T.C16[:, 20:28], l4, Op.add, 2.0, Op.add)
-    t_qu = quant("QU", 0, 128, T.UT[:], [du])
-    t_uc = run("v", lambda q: q.tensor_copy(T.UU[:].bitcast(dt.uint32), T.QU[:].bitcast(dt.uint32).indirect(T.PU[:])), [t_qu, t_pu])
-    t_us = run("a", lambda q: q.activation(T.UUs[:], T.QUs[:].indirect(T.PU[:]), Fn.Copy), [t_qu, t_pu])
-    t_qn = quant("QN", 0, 128, T.BT[:], [t_bt])
-    for t in range(3):
-        dma("sy", T["G%d" % t][:, 112:128].bitcast(dt.uint8), T.QN[:, 112:128].bitcast(dt.uint8), "dn", [t_qn])
-        t_gn = dma("sy", T["G%ds" % t][:, 112:128], T.QNs[:, 112:128], "dn")
 
-    def coefficients(put, name, i):
-        j = 0
+    def coefficients(name, i):
+        runs, j = [], 0
         while j < NL:
             e = j
             while e < NL and LIN[e][i] == LIN[j][i]:
                 e += 1
-            tok = put(T[name][:, j:e], float(LIN[j][i]), e - j)
+            if LIN[j][i] != 0:
+                runs.append((T[name][:, j:e], float(LIN[j][i]), e - j))
             j = e
+        return runs
+
+    def put(runs):
+        for ap, value, n in runs:
+            tok = affine(ap, T.NIL[:, 0:n], value, deps=[t_nil])
         return tok
 
-    def by_scalar(ap, value, n):
-        return run("a", lambda q: q.activation(ap, T.NIL[:, 0:n], Fn.Identity, bias=value), [t_nil])
-
-    t_be = coefficients(by_scalar, "BE", 1)
-    t_ga = coefficients(by_scalar, "GA", 2)
-    t_edb = acopy(T.EDB[:], T.ED[:], [t_ed], scale=64.0)
-
-    def later_constants():
-        ta = coefficients(lambda ap, value, n: fill(ap, value), "AL", 0)
-        for b in range(4):
-            te = quant("EB", 128 * b, 128 * b + 128, T.EDB[:, 3 - b:515 - b], [t_edb])
-        ts(T.TP[:], T.C16[:, 0:20], lane, Op.add)
-        t1 = ts(T.JF[:, 0:8], T.JF[:, 0:8], lane, Op.add, deps=[t_jf])
-        t2 = ts(T.JF[:, 8:56], T.JF[:, 8:56], l1, Op.add)
-        t3 = ts(T.JF[:, 56:76], T.JF[:, 56:76], lane, Op.add)
-        ts(T.TN[:], T.TP[:], -1.0, Op.mult, deps=[t1])
-        vcopy(T.JI[:], T.JF[:], [t3])
-        t4 = ts(T.IA[:], T.JF[:], -1.0, Op.mult, 319.0, Op.add)
-        t5 = ts(T.IB[:], T.IA[:], 1, Op.bitwise_and, deps=[t4])
-        t6 = ts(T.IC[:], T.IA[:], 1, Op.logical_shift_right)
-        t7 = ts(T.EI[:], T.IB[:], -2.0, Op.mult, 1.0, Op.add, deps=[t5])
-        t8 = ts(T.EJ[:], T.IC[:], 0.5, Op.add, deps=[t6])
-        t9 = tt(T.EP[:], T.EI[:], T.EJ[:], Op.mult, deps=[t7, t8])
-        return [ta, t9, t_be, t_ga], te
-
+    t_ab = put(coefficients("AL", 0) + coefficients("BE", 1))
+    ga = coefficients("GA", 2)
+    t_pu = vcopy(T.PU[:], T.PO[:], [t_po])
+    for i, m in ((1, 15), (2, 12), (3, 12), (4, 3), (5, 1)):
+        ts(T.LI[:, i:i + 1], T.LI[:, 0:1], m, Op.bitwise_and, deps=[t_li])
+    t_l6 = ts(T.LI[:, 6:7], T.LI[:, 0:1], 2, Op.logical_shift_right, 1, Op.bitwise_and)
+    fill(T.LTC[:, 65:66], 512.0)
+    t_lt = fill(T.LTK[:, 25:26], 320.0)
+    t_lane = vcopy(T.LANE[:], T.LI[:], [t_l6])
+    t_bt = fill(T.BT[:], 0.0)
+    t_l1 = ts(T.LANE[:, 3:4], T.LANE[:, 2:3], 0.25, Op.mult, deps=[t_lane])
+    ts(T.LANE[:, 4:5], T.LANE[:, 4:5], 320.0, Op.mult)
+    ts(T.LAN2[:, 0:2], T.LANE[:, 5:7], -1.0, Op.mult, 0.5, Op.add)
+    t_lan2 = ts(T.LAN2[:, 2:4], T.LANE[:, 5:7], 319.5, Op.mult, -159.5, Op.add)
+    lane, l4, l1, b320 = (T.LANE[:, i:i + 1] for i in (1, 2, 3, 4))
+    t_tjb = ts(T.TJB[:], T.C16[:], lane, Op.add, float(PAD), Op.add, [t_c16, t_l1])
+    ts(T.Z4[:], T.C16[:, 20:28], l4, Op.add)
+    t_cz = ts(T.CZ[:], T.C16[:, 20:28], l4, Op.add, 2.0, Op.add)
     for b in range(4):
         t_eh = quant("EH", 128 * b, 128 * b + 128, T.ED[:, 3 - b:515 - b], [t_ed])
+    t_qu = quant("QU", 0, 128, T.UT[:], [du])
+    t_us = run("a", lambda q: q.activation(T.UUs[:], T.QUs[:].indirect(T.PU[:]), Fn.Copy), [t_qu, t_pu])
+    t_uc = run("v", lambda q: q.tensor_copy(T.UU[:].bitcast(dt.uint32), T.QU[:].bitcast(dt.uint32).indirect(T.PU[:])), [t_qu, t_pu])
+    t_edb = acopy(T.EDB[:], T.ED[:], [t_ed], scale=64.0)
+    put(ga[:6])
+
+    def a_constants():
+        put(ga[6:])
+        affine(T.TP[:], T.C16[:, 0:20], lane, deps=[t_c16, t_tjb, t_lan2, t_jf])
+        affine(T.JF[:, 0:8], T.JF[:, 0:8], lane)
+        affine(T.JF[:, 8:56], T.JF[:, 8:56], l1)
+        j = affine(T.JF[:, 56:76], T.JF[:, 56:76], lane)
+        affine(T.TN[:], T.TP[:], 0.0, -1.0, [j])
+        for lo, hi, i in ((0, 8, 0), (8, 56, 1), (56, 76, 0)):
+            e = affine(T.EP[:, lo:hi], T.JF[:, lo:hi], T.LAN2[:, 2 + i:3 + i], T.LAN2[:, i:i + 1], [j])
+        return [e], j
 
     CK, FV, SMT, WA, WO = T.CK, T.FV, T.SM, T.WA, T.WO
-    C4, K4 = CK[:, 0:1], CK[:, 1:2]
+    C4, K4, fv = CK[:, 0:1], CK[:, 1:2], SMT[:, 0:1]
 
     def sc(name):
         i = SCOL[name]
         return FV[:, i:i + 1] if i < NF else T.S4[:, i:i + 1]
 
-    def lists(last, t_ck, t_const):
+    def lists(last, t_s, t_const, copies):
         o = (56, 76) if last else (0, 56)
         w = o[1] - o[0]
         J, JI, E, P = T.JF[:, o[0]:o[1]], T.JI[:, o[0]:o[1]], T.EP[:, o[0]:o[1]], T.TP[:]
         wa = lambda i: WA[:, 20 * i:20 * i + 20]
         wo = lambda i: WO[:, 64 * i:64 * i + w]
         it = lambda n: T[n][:, 0:w]
-        k = {"ck": t_ck, "con": t_const}
+        k = {"s": t_s, "con": t_const}
 
         def step(name, fn, *deps):
             k[name] = fn([x for d in deps for x in (k[d] if isinstance(k[d], list) else [k[d]])])
 
-        fv = SMT[:, 0:1]
-        step("f", lambda d: ts(fv, C4, 640.0, Op.is_lt, deps=d), "ck")
-        step("s1", lambda d: ts(T.S1[:], T.AL[:], C4, Op.mult, 0.25, Op.mult, d), "ck", "con")
-        step("s2", lambda d: ts(T.S2[:], T.BE[:], K4, Op.mult, 0.25, Op.mult, d), "ck", "con")
-        step("s3", lambda d: tt(T.S3[:], T.S1[:], T.GA[:], Op.add, d), "s1")
-        step("s4", lambda d: tt(T.S4[:], T.S3[:], T.S2[:], Op.add, d), "s3", "s2")
-        step("fs", lambda d: ts(T.FS[:], T.S4[:, NF + NN:NL], fv, Op.mult, deps=d), "s4", "f")
+        step("s3", lambda d: tt(T.S3[:], T.S1[:], T.GA[:], Op.add, d), "s", "con")
+        step("s4", lambda d: tt(T.S4[:], T.S3[:], T.S2[:], Op.add, d), "s3")
+        step("fs", lambda d: ts(T.FS[:], T.S4[:, NF + NN:NL], fv, Op.mult, deps=d), "s4")
+        step("m1", lambda d: ts(wa(0), P, sc("ck"), Op.is_ge, sc("n2n"), Op.mult, d), "s4")
+        step("fv", lambda d: tt(FV[:], T.FS[:], T.S4[:, 0:NF], Op.add, d), "fs")
+        step("m2", lambda d: ts(wa(1), P, sc("c"), Op.is_ge, sc("X1"), Op.mult, d), "s4")
+        step("ge", lambda d: ts(SMT[:, 5:6], sc("de"), 0.0, Op.is_ge, deps=d), "fv")
+        step("hm", lambda d: ts(SMT[:, 6:7], sc("de"), 0.0, Op.is_lt, deps=d), "fv")
+        step("gxz", lambda d: ts(SMT[:, 8:10], FV[:, SCOL["X"]:SCOL["Z"] + 1], SMT[:, 5:6], Op.mult, deps=d), "ge")
+        copies(2)
+        step("w", lambda d: affine(wa(6), P, sc("tau"), 2.0, d), "fv")
+        step("e1", lambda d: affine(wo(4), J, SMT[:, 9:10], SMT[:, 8:9], d), "gxz")
+        step("e2", lambda d: affine(wo(5), E, 0.0, SMT[:, 6:7], d), "hm")
+        copies(4)
         ops_a = [
-            ("m1", lambda d: ts(wa(0), P, sc("ck"), Op.is_ge, sc("n2n"), Op.mult, d), "s4"),
-            ("m2", lambda d: ts(wa(1), P, sc("c"), Op.is_ge, sc("X1"), Op.mult, d), "s4"),
             ("m4x", lambda d: ts(wa(3), P, sc("cpk"), Op.is_ge, sc("k2n"), Op.mult, d), "s4"),
             ("a1", lambda d: tt(wa(8), wa(0), T.TN[:], Op.add, d), "m1"),
             ("RB", lambda d: ts(SMT[:, 2:4], FV[:, 0:2], sc("c"), Op.max, deps=d), "fv"),
             ("r2", lambda d: ts(wa(5), P, sc("R1"), Op.is_lt, deps=d), "fv"),
-            ("w", lambda d: ts(wa(6), P, 2.0, Op.mult, sc("tau"), Op.add, d), "fv"),
             ("m3", lambda d: ts(wa(2), P, SMT[:, 3:4], Op.is_ge, sc("n2n"), Op.mult, d), "RB"),
             ("r1", lambda d: ts(wa(4), P, SMT[:, 2:3], Op.is_ge, deps=d), "RB"),
-            ("rw", lambda d: tt(wa(7), wa(5), wa(6), Op.mult, d), "r2", "w"),
             ("a2", lambda d: tt(wa(9), wa(1), wa(2), Op.add, d), "m2", "m3"),
-            ("rv", lambda d: tt(wa(10), wa(4), wa(7), Op.mult, d), "r1", "rw"),
+            ("rw", lambda d: tt(wa(7), wa(5), wa(4), Op.mult, d), "r2", "r1"),
             ("a4", lambda d: tt(wa(11), wa(8), wa(9), Op.add, d), "a1", "a2"),
-            ("a3", lambda d: tt(wa(12), wa(10), wa(3), Op.add, d), "rv", "m4x"),
-            ("a5", lambda d: tt(wa(13), wa(11), wa(12), Op.add, d), "a4", "a3"),
+            ("rv", lambda d: tt(wa(10), wa(6), wa(7), Op.mult, d), "w", "rw"),
+            ("a6", lambda d: tt(wa(12), wa(11), wa(3), Op.add, d), "a4", "m4x"),
+            ("a5", lambda d: tt(wa(13), wa(10), wa(12), Op.add, d), "rv", "a6"),
             ("LA", lambda d: ts(T.LA[:], wa(13), sc("base"), Op.add, deps=d), "a5"),
         ]
         ops_o = [
-            ("fv", lambda d: tt(FV[:], T.FS[:], T.S4[:, 0:NF], Op.add, d), "fs"),
             ("t", lambda d: ts(wo(0), J, sc("m4"), Op.subtract, 0.0, Op.max, d), "fv"),
             ("mx", lambda d: tt(SMT[:, 4:5], sc("de"), sc("d2"), Op.max, d), "fv"),
             ("Q", lambda d: ts(it("OQ"), wo(0), fv, Op.subtract, 1.0 / 3.0, Op.mult, d), "t"),
-            ("ge", lambda d: ts(SMT[:, 5:6], sc("de"), 0.0, Op.is_ge, deps=d), "fv"),
-            ("s", lambda d: tt(it("OS"), it("OQ"), JI, Op.add, d), "Q"),
-            ("hm", lambda d: ts(SMT[:, 6:7], sc("de"), 0.0, Op.is_lt, deps=d), "fv"),
-            ("b1", lambda d: ts(it("O1"), it("OS"), 1, Op.logical_shift_right, 1, Op.bitwise_and, d), "s"),
-            ("z", lambda d: ts(it("OZ"), it("OS"), 2, Op.logical_shift_right, deps=d), "s"),
-            ("b0", lambda d: ts(it("O0"), it("OS"), 1, Op.bitwise_and, deps=d), "s"),
+            ("mk", lambda d: ts(wo(8), J, SMT[:, 4:5], Op.add, 320.0, Op.is_ge, d), "mx"),
+            ("s5", lambda d: tt(it("OS"), it("OQ"), JI, Op.add, d), "Q"),
+            ("b1", lambda d: ts(it("O1"), it("OS"), 1, Op.logical_shift_right, 1, Op.bitwise_and, d), "s5"),
+            ("z", lambda d: ts(it("OZ"), it("OS"), 2, Op.logical_shift_right, deps=d), "s5"),
+            ("b0", lambda d: ts(it("O0"), it("OS"), 1, Op.bitwise_and, deps=d), "s5"),
             ("sk", lambda d: ts(wo(1), it("O1"), sc("k2"), Op.mult, sc("kh"), Op.add, d), "b1"),
-            ("gxz", lambda d: ts(SMT[:, 8:10], FV[:, SCOL["X"]:SCOL["Z"] + 1], SMT[:, 5:6], Op.mult, deps=d), "ge"),
             ("s12", lambda d: ts(wo(2), it("O0"), -2.0, Op.mult, 1.0, Op.add, d), "b0"),
             ("u", lambda d: tt(wo(3), wo(1), it("OZ"), Op.add, d), "sk", "z"),
-            ("e1", lambda d: ts(wo(4), J, SMT[:, 8:9], Op.mult, SMT[:, 9:10], Op.add, d), "gxz"),
-            ("e2", lambda d: ts(wo(5), E, SMT[:, 6:7], Op.mult, deps=d), "hm"),
-            ("p12", lambda d: tt(wo(6), wo(2), wo(3), Op.mult, d), "s12", "u"),
             ("p3", lambda d: tt(wo(7), wo(4), wo(5), Op.add, d), "e1", "e2"),
-            ("mk", lambda d: ts(wo(8), J, SMT[:, 4:5], Op.add, 320.0, Op.is_ge, d), "mx"),
+            ("p12", lambda d: tt(wo(6), wo(2), wo(3), Op.mult, d), "s12", "u"),
             ("df", lambda d: tt(wo(9), wo(7), wo(6), Op.subtract, d), "p3", "p12"),
             ("dm", lambda d: tt(wo(10), wo(9), wo(8), Op.mult, d), "df", "mk"),
             ("pl", lambda d: tt(wo(11), wo(10), wo(6), Op.add, d), "dm"),
@@ -259,39 +252,40 @@ def rank_program(g, core, T, topo):
             ops_o.append(("LOx", lambda d: ts(T.LO[:, 0:8], WO[:, 704:712], sc("cm"), Op.add, deps=d), "pl"))
             ops_o.append(("LO", lambda d: ts(T.LO[:, 8:56], WO[:, 712:760], sc("cm"), Op.add, b320, Op.add, d), "pl"))
         na, no = len(ops_a), len(ops_o)
-        i = 0
-        for j in range(no):
-            step(*ops_o[j])
-            while i < na and (i + 1) * no <= (j + 1) * na:
-                step(*ops_a[i])
-                i += 1
+        for j in range(max(na, no)):
+            if j < no:
+                step(*ops_o[j])
+            if j < na:
+                step(*ops_a[j])
         return k["LA"], k["LO"]
 
-    first, rest = [dx], [dx, t_pad0]
+    first, rest, tail = [dx], [dx, t_pad0], None
     for t in range(3):
         X, last = T["X%d" % t], t == 2
         t_qs = quant("QS", 0, 128, X[:, PAD + 320:PAD + 832], first)
-        if t == 0:
-            t_s1 = mm(6, 128, "UU", 0, "QS", 0, [t_qs, t_uc, t_us])
-        else:
-            t_s1 = mm(6, 128, "UU", 0, "QS", 0, [t_qs])
+        t_s1 = mm(6, 128, "UU", 0, "QS", 0, [t_qs, t_uc, t_us])
         t_s2 = mm(7, 128, "UU", 128, "QS", 0)
+        if tail:
+            rest = rest + [tail()]
         t1 = run("v", lambda q: q.tensor_tensor_scan(T.RMC[:], T.NIL[:, 0:65], bank(6, 48, 113), -1e29, Op.add, Op.max), [t_s1, t_nil])
         t2 = run("v", lambda q: q.tensor_tensor_scan(T.RMK[:], T.NIL[:, 0:25], bank(7, 0, 25), -1e29, Op.add, Op.max), [t_s2])
         t3 = ts(T.LTC[:, 0:65], T.RMC[:], T.RMC[:, 64:65], Op.is_lt, 4.0, Op.mult, [t1])
         t4 = ts(T.LTK[:, 0:25], T.RMK[:], T.RMK[:, 24:25], Op.is_lt, 4.0, Op.mult, [t2])
         t5 = run("v", lambda q: q.tensor_reduce(C4, T.LTC[:], AxisListType.X, Op.add), [t3, t_lt])
         t6 = run("v", lambda q: q.tensor_reduce(K4, T.LTK[:], AxisListType.X, Op.add), [t4])
-        t_l1 = ts(T.L1[:], T.TJB[:, 0:20], C4, Op.add, K4, Op.subtract, [t5, t6, t_tjb])
-        t_b1 = acopy(T.BT[:, 0:320], X[:].indirect(T.L1[:]), [t_l1, t_qn] + rest)
         w2 = lambda i: T.W2[:, 8 * i:8 * i + 8]
-        fm, kf = T.SM[:, 12:13], T.SM[:, 13:14]
-        t7 = ts(fm, C4, 640.0, Op.is_ge, -1.0, Op.mult)
-        t8 = ts(w2(0), T.Z4[:], K4, Op.is_ge, 2.0, Op.mult, [t_cz])
+        fm, kf = SMT[:, 12:13], SMT[:, 13:14]
+        t7 = ts(fm, C4, 640.0, Op.is_ge, -1.0, Op.mult, [t5])
+        t_l1 = ts(T.L1[:], T.TJB[:, 0:20], C4, Op.add, K4, Op.subtract, [t6, t_tjb])
+        t_b1 = acopy(T.BT[:, 0:320], X[:].indirect(T.L1[:]), [t_l1, t_bt] + rest)
         t9 = ts(kf, fm, 1.0, Op.add, K4, Op.mult, [t7])
+        t8 = ts(w2(0), T.Z4[:], K4, Op.is_ge, 2.0, Op.mult, [t_cz])
         t10 = ts(w2(1), T.CZ[:], fm, Op.mult, kf, Op.add, [t9])
+        ts(fv, C4, 640.0, Op.is_lt)
         t11 = tt(w2(2), w2(0), w2(1), Op.mult, [t8, t10])
+        ts(T.S1[:], T.AL[:], C4, Op.mult, 0.25, Op.mult, [t_ab])
         t12 = tt(w2(3), w2(2), T.TJB[:, 20:28], Op.add, [t11])
+        t_s = ts(T.S2[:], T.BE[:], K4, Op.mult, 0.25, Op.mult)
         t_l2 = ts(T.L2[:], w2(3), C4, Op.add, K4, Op.subtract, [t12])
         t_b2 = vcopy(T.BT[:, 320:448], X[:].indirect(T.L2[:]), [t_l2] + rest)
         B, G = "B%d" % t, "G%d" % t
@@ -306,68 +300,105 @@ def rank_program(g, core, T, topo):
         total["arr%d" % t] = 2 * len(topo.engines(nxt, core)[:8])
         t_qx = quant("QX", 0, 320, X[:, PAD:PAD + 1280], rest)
         if t == 0:
-            t_con, t_eb = later_constants()
-        for b in range(4):
-            t_hf = mm(b, 320, "EH", 128 * b, "QX", 0, [t_qx, t_eh])
-            t_f = acopy(T.PL[:, 432 * b:432 * b + 320], bank(b, 0, 320), [t_hf])
-            if b < 2:
-                t_pl = acopy(T.FP[:, 320 * b:320 * b + 320], bank(b, 0, 320))
+            for i in range(3):
+                dma("sy", T["G%d" % i][:, 112:128].bitcast(dt.uint8), T.B0[:, 112:128].bitcast(dt.uint8), "dn", [t_qb])
+                t_gn = dma("sy", T["G%ds" % i][:, 112:128], T.B0s[:, 112:128], "dn")
+            t_con, t_j = a_constants()
+            for n in ("X1", "X2"):
+                for o in (0, PAD + 1280):
+                    t_pad = iota(T[n][:, o:o + PAD], [[0, PAD]], 0, 0)
+            t_iot = iota(T.IOT[:], [[1, 320]], 0, 0)
+            for b in range(4):
+                t_eb = quant("EB", 128 * b, 128 * b + 128, T.EDB[:, 3 - b:515 - b], [t_edb])
+            t_con.append(vcopy(T.JI[:], T.JF[:], [t_j]))
+        t_hf = [mm(b, 320, "EH", 128 * b, "QX", 0, [t_qx, t_eh]) for b in range(4)]
+        done = {}
+
+        def copies(n):
+            for b in range(n - 2, n):
+                done[b] = acopy(T.PL[:, 432 * b:432 * b + 320], bank(b, 0, 320), [t_hf[b]])
+                if b < 2:
+                    done[b] = acopy(T.FP[:, 320 * b:320 * b + 320], bank(b, 0, 320))
+
+        t_la, t_lo = lists(last, [t_s], t_con, copies)
         for b in range(2):
-            mm(b, 320, "EB", 128 * b, "QX", 0, [t_pl, t_eb], stop=False)
-        t_la, t_lo = lists(last, [t5, t6], t_con)
+            mm(RBANK[0][b], 160, "EB", 128 * b, "QX", 0, [done[b], t_eb], stop=False)
         if t == 0:
             t_qv = quant("QV", 0, 128, T.VT[:], [dv])
         if last:
             t_lor = run("a", lambda q: q.activation(T.LOR[:], T.IOT[:].indirect(T.LO[:, 0:20]), Fn.Copy), [t_lo, t_iot])
             dma("sy", T.lo[:], T.LOR[0:128:16, :], "out", [t_lor])
-        arr = [("arr%d" % t, total["arr%d" % t]), t_gn]
-        t_g0 = mm(4, 128, "EH", 0, G, 0, arr)
-        t_g2 = mm(5, 128, "EH", 256, G, 0)
-        t_g1 = mm(6, 128, "EH", 128, G, 0)
-        t_g3 = mm(7, 128, "EH", 384, G, 0)
+        t_g = {}
+        for b, bk in ((0, 4), (2, 5), (1, 6), (3, 7)):
+            t_g[b] = mm(bk, 128, "EH", 128 * b, G, 0, [("arr%d" % t, total["arr%d" % t]), t_gn])
         win = lambda b: T.PL[:, 432 * b:432 * b + 432]
-        t_c0 = vcopy(T.PL[:, 320:432], bank(4, 0, 112), [t_g0])
-        t_c2 = acopy(T.PL[:, 1184:1296], bank(5, 0, 112), [t_g2])
-        t_c1 = vcopy(T.PL[:, 752:864], bank(6, 0, 112), [t_g1])
-        t_a2 = acopy(T.AB[:, 0:320], win(2).indirect(T.LA[:]), [t_la, t_c2])
-        t_c3 = acopy(T.PL[:, 1616:1728], bank(7, 0, 112), [t_g3])
-        t_a3 = acopy(T.AB[:, 320:640], win(3).indirect(T.LA[:]), [t_c3])
-        mm(4, 320, "EB", 256, "QX", 0, [t_c0], stop=False)
-        mm(5, 320, "EB", 384, "QX", 0, [t_c2], stop=False)
-        tt(T.ZT[:, 0:1280:4], win(0).indirect(T.LA[:]), T.FP[:, 0:320], Op.add, [t_c0, t_f, t_la])
-        tt(T.ZT[:, 1:1280:4], win(1).indirect(T.LA[:]), T.FP[:, 320:640], Op.add, [t_c1])
-        tt(T.ZT[:, 2:1280:4], bank(2, 0, 320), T.AB[:, 0:320], Op.add, [t_a2])
-        t_z = tt(T.ZT[:, 3:1280:4], bank(3, 0, 320), T.AB[:, 320:640], Op.add, [t_a3])
-        t_qz = quant("QZ", 0, 320, T.ZT[:], [t_z])
-        t_r = [mm((0, 1, 4, 5)[b], 320, "QW", 128 * b, "QZ", 0, [t_qz, dw], start=False) for b in range(4)]
-        XN = T["X%d" % (t + 1)]
-        new = []
+        late = lambda b: T.PL[:, 432 * b + 320:432 * b + 432]
+        la = lambda h: T.LA[:, 10 * h:10 * h + 10]
+        zt = lambda b, h: T.ZT[:, 640 * h + b:640 * h + 640:4]
+        fp = lambda b, h: T.FP[:, 320 * b + 160 * h:320 * b + 160 * h + 160]
+        ab = lambda b, h: T.AB[:, 320 * (b - 2) + 160 * h:320 * (b - 2) + 160 * h + 160]
+        t_c, t_a = {}, {}
+        t_c[2] = acopy(late(2), bank(5, 0, 112), [t_g[2]])
+        t_a[2, 0] = acopy(ab(2, 0), win(2).indirect(la(0)), [t_la, t_c[2]])
+        t_c[3] = acopy(late(3), bank(7, 0, 112), [t_g[3]])
+        t_a[3, 0] = acopy(ab(3, 0), win(3).indirect(la(0)), [t_c[3]])
+        t_a[2, 1] = acopy(ab(2, 1), win(2).indirect(la(1)))
+        t_a[3, 1] = acopy(ab(3, 1), win(3).indirect(la(1)))
+        t_c[0] = vcopy(late(0), bank(4, 0, 112), [t_g[0]])
+        tt(zt(0, 0), win(0).indirect(la(0)), fp(0, 0), Op.add, [t_c[0], done[3], t_la])
+        t_c[1] = vcopy(late(1), bank(6, 0, 112), [t_g[1]])
+        tt(zt(1, 0), win(1).indirect(la(0)), fp(1, 0), Op.add, [t_c[1]])
+        mm(RBANK[0][2], 160, "EB", 256, "QX", 0, [t_c[0]], stop=False)
+        mm(RBANK[0][3], 160, "EB", 384, "QX", 0, [t_c[2]], stop=False)
+        mm(RBANK[1][0], 160, "EB", 0, "QX", 160, [t_c[1]], stop=False)
+        mm(RBANK[1][1], 160, "EB", 128, "QX", 160, [t_c[3]], stop=False)
+        tt(zt(2, 0), bank(2, 0, 160), ab(2, 0), Op.add, [t_a[2, 0]])
+        t_z = tt(zt(3, 0), bank(3, 0, 160), ab(3, 0), Op.add, [t_a[3, 0]])
+        t_qz = quant("QZ", 0, 160, T.ZT[:, 0:640], [t_z])
+        tt(zt(0, 1), win(0).indirect(la(1)), fp(0, 1), Op.add)
+        tt(zt(1, 1), win(1).indirect(la(1)), fp(1, 1), Op.add)
+        t_z2 = tt(zt(2, 1), bank(2, 160, 320), ab(2, 1), Op.add, [t_a[2, 1]])
+        t_z3 = tt(zt(3, 1), bank(3, 160, 320), ab(3, 1), Op.add, [t_a[3, 1]])
+        t_qz2 = quant("QZ", 160, 320, T.ZT[:, 640:1280], [t_z3])
+        yp = lambda b, h: T.YP[:, 320 * b + 160 * h:320 * b + 160 * h + 160]
+        t_r = [mm(RBANK[0][b], 160, "QW", 128 * b, "QZ", 0, [t_qz, dw], start=False) for b in range(4)]
+        mm(2, 160, "EB", 256, "QX", 160, [t_z2], stop=False)
+        mm(3, 160, "EB", 384, "QX", 160, [t_z3], stop=False)
+        t_r2 = [mm(RBANK[1][b], 160, "QW", 128 * b, "QZ", 160, [t_qz2], start=False) for b in range(4)]
+        new = [acopy(yp(b, 0), bank(RBANK[0][b], 0, 160), [t_r[b]], scale=0.03125) for b in range(4)]
+        XN, YP, LO = T["X%d" % (t + 1)], T.YP, T.LO
         for b in range(4):
-            src, yp = bank((0, 1, 4, 5)[b], 0, 320), T.YP[:, 320 * b:320 * b + 320]
+            src, copy = bank(RBANK[1][b], 0, 160), (vcopy, acopy)[b % 2]
             if b % 2 == 0:
-                ty = ts(yp, src, 0.03125, Op.mult, deps=[t_r[b]])
+                ty = ts(yp(b, 1), src, 0.03125, Op.mult, deps=[t_r2[b]])
             else:
-                ty = acopy(yp, src, [t_r[b]], scale=0.03125)
+                ty = acopy(yp(b, 1), src, [t_r2[b]], scale=0.03125)
+            plane, deps = YP[:, 320 * b:320 * b + 320], [ty, new[b], t_lo]
             new.append(ty)
-            copy = vcopy if b % 2 == 0 else acopy
             if last:
-                new.append(copy(XN[:, b:1280:4], yp.indirect(T.LO[:, 0:20]), [ty, t_lo]))
+                new.append(copy(XN[:, b:640:4], plane.indirect(LO[:, 0:10]), deps))
             else:
-                new.append(copy(XN[:, PAD + 320 + b:PAD + 832:4], yp.indirect(T.LO[:, 0:8]), [ty, t_lo]))
+                new.append(copy(XN[:, PAD + 320 + b:PAD + 832:4], plane.indirect(LO[:, 0:8]), deps))
         first = list(new)
         if not last:
-            r1 = acopy(XN[:, PAD:PAD + 320], T.YP[:].indirect(T.LO[:, 8:28]), new)
-            r2 = acopy(XN[:, PAD + 832:PAD + 1280], T.YP[:].indirect(T.LO[:, 28:56]))
+            r1 = acopy(XN[:, PAD + 832:PAD + 1280], YP[:].indirect(LO[:, 28:56]), new)
+            r2 = acopy(XN[:, PAD + 128:PAD + 320], YP[:].indirect(LO[:, 16:28]))
+            tail = lambda XN=XN, new=new: vcopy(XN[:, PAD:PAD + 128], T.YP[:].indirect(T.LO[:, 8:16]), new)
             rest = new + [r1, r2, t_pad]
 
-    t_qf = quant("QF", 0, 320, T.X3[:], first)
-    t_y0 = mm(2, 160, "QV", 0, "QF", 0, [t_qf, t_qv])
-    t_y1 = mm(3, 160, "QV", 0, "QF", 160)
-    dma("sy", T.oc[:], T.QF[:].bitcast(dt.uint8), "out", [t_qf])
-    t_o0 = vcopy(T.YO[:, 0:160], bank(2, 0, 160), [t_y0])
-    t_o1 = acopy(T.YO[:, 160:320], bank(3, 0, 160), [t_y1])
+    second = []
+    for b in range(4):
+        second.append((vcopy, acopy)[b % 2](XN[:, 640 + b:1280:4], YP[:, 320 * b:320 * b + 320].indirect(LO[:, 10:20]), new))
+        if b == 0:
+            t_q0 = quant("QF", 0, 160, XN[:, 0:640], first)
+    t_q1 = quant("QF", 160, 320, XN[:, 640:1280], second)
+    t_y0 = mm(2, 160, "QV", 0, "QF", 0, [t_q0, t_qv])
+    t_y1 = mm(3, 160, "QV", 0, "QF", 160, [t_q1])
+    t_o0 = acopy(T.YO[:, 0:160], bank(2, 0, 160), [t_y0])
+    dma("a", T.y[:, 0:160], T.YO[:, 0:160], "out", [t_o0])
+    dma("sy", T.oc[:], T.QF[:].bitcast(dt.uint8), "out", [t_q0, t_q1])
     for k in range(4):
-        dma("sy" if k < 2 else "a", T.osc[4 * k:4 * k + 4, :], T.QFs[32 * k:32 * k + 4, :], "out", [t_qf])
-    dma("sy", T.y[:, 0:160], T.YO[:, 0:160], "out", [t_o0])
-    dma("a", T.y[:, 160:320], T.YO[:, 160:320], "out", [t_o1])
+        dma("a" if k < 2 else "sy", T.osc[4 * k:4 * k + 4, :], T.QFs[32 * k:32 * k + 4, :], "out", [t_q0, t_q1])
+    t_o1 = vcopy(T.YO[:, 160:320], bank(3, 0, 160), [t_y1])
+    dma("sy", T.y[:, 160:320], T.YO[:, 160:320], "out", [t_o1])
     wait("gc", list(total.items()))

@@ -1,8 +1,11 @@
 import numpy as np
 from concourse.mybir import AluOpType as Op, AxisListType, ActivationFunctionType as Fn, dt
 
-PAD = 256
-XW = 1280 + 2 * PAD
+NZ = 256
+PAD = 128 + NZ
+XW = PAD + 1280
+WIN = PAD + 832
+PART = ((0, 192), (192, 320))
 FCOLS = [
     ("R0", (0, 2, 0), (2, -2, 0)), ("B1", (2, 2, -320), (0, 0, 0)),
     ("R1", (2, 2, -320), (-2, -2, 1320)), ("tau", (-1, -3, -319), (-2, 2, 640)),
@@ -21,7 +24,7 @@ SCOL = {n: i for i, n in enumerate([n for n, _, _ in FCOLS] + [n for n, _ in NCO
 F8, U8, BF, F32, I32, U16 = "float8_e4m3fn_x4", "uint8", "bfloat16", "float32", "int32", "uint16"
 SCRATCH = {"PS": ("psum", [128, 4096], F32)}
 for _n, _w in (("X0", XW), ("X1", XW), ("X2", XW), ("X3", 1280), ("UT", 512), ("VT", 512), ("BT", 512), ("ZT", 1280), ("PL", 1728),
-               ("FP", 640), ("AB", 640), ("YP", 1280), ("ED", 516), ("EDB", 516), ("HALF", 516)):
+               ("FP", 640), ("AB", 1280), ("YP", 1280), ("ED", 516), ("EDB", 516), ("HALF", 516)):
     SCRATCH[_n] = ("sbuf", [128, _w], BF)
 for _n, _w in (("QU", 128), ("UU", 256), ("QV", 128), ("QW", 512), ("EH", 512), ("EB", 512), ("QS", 128), ("QX", 320), ("QZ", 320),
                ("QF", 320), ("B0", 128), ("B1", 128), ("B2", 128), ("G0", 128), ("G1", 128), ("G2", 128)):
@@ -35,8 +38,9 @@ for _n, _w in (("LI", 7), ("JI", 76), ("PO", 16), ("OQ", 56), ("OS", 56), ("O0",
     SCRATCH[_n] = ("sbuf", [128, _w], I32)
 for _n, _w in (("PU", 16), ("L1", 20), ("L2", 8), ("LA", 20), ("LO", 56)):
     SCRATCH[_n] = ("sbuf", [128, _w], U16)
-SEMAPHORES = ["v", "a", "te", "gc", "dx", "du", "dv", "dw", "dn", "out", "arr0", "arr1", "arr2", "sent"]
+SEMAPHORES = ["v", "a", "te", "gc", "dx", "dy", "du", "dv", "dw", "dn", "out", "arr0", "arr1", "arr2", "sent"]
 RBANK = ((0, 1, 4, 5), (6, 7, 2, 3))
+GBANK = (4, 6, 5, 7)
 
 
 def rank_program(g, core, T, topo):
@@ -94,6 +98,10 @@ def rank_program(g, core, T, topo):
         return run("te", lambda q: q.matmul_mx(T.PS[:, 512 * bank:512 * bank + n], T[w][:, wlo:wlo + 128], T[w + "s"][:, wlo:wlo + 128],
                                                T[x][:, xlo:xlo + n], T[x + "s"][:, xlo:xlo + n], start, stop), deps)
 
+    def part(h, b, w, x, deps, start, stop):
+        lo, hi = PART[h]
+        return mm(RBANK[h][b], hi - lo, w, 128 * b, x, lo, deps, start, stop)
+
     def bank(b, lo, hi):
         return T.PS[:, 512 * b + lo:512 * b + hi]
 
@@ -105,8 +113,9 @@ def rank_program(g, core, T, topo):
             return run("gc", lambda q: q.iota(ap, pattern, base, cm, allow_small_or_imprecise_dtypes=True))
         return run("gc", lambda q: q.iota(ap, pattern, base, cm))
 
-    dx = dma("sy", T.X0[:, PAD:PAD + 1280], T.x[:], "dx")
+    dx = dma("sy", T.X0[:, PAD:XW], T.x[:], "dx")
     du = dma("a", T.UT[:], T.u[:], "du")
+    dy = dma("sy", T.X0[:, 0:128], T.x[:, 1152:1280], "dy")
     dma("sy", T.QW[:].bitcast(dt.uint8), T.wc[:], "dw")
     dw = dma("sy", T.QWs[:], T.ws[:], "dw")
     dv = dma("sy", T.VT[:], T.v[:], "dv")
@@ -120,8 +129,7 @@ def rank_program(g, core, T, topo):
     t_nil = fill(T.GA[:], 0.0)
     t_half = fill(T.HALF[:], 0.5)
     t_ed = run("gc", lambda q: q.affine_select(T.ED[:], T.HALF[:], [[-1, 516]], Op.is_equal, 0.0, 3, 4), [t_half])
-    for o in (0, PAD + 1280):
-        t_pad0 = iota(T.X0[:, o:o + PAD], [[0, PAD]], 0, 0)
+    t_pad0 = iota(T.X0[:, 128:PAD], [[0, NZ]], 0, 0)
     iota(T.JF[:, 0:8], [[16, 8]], 80, 0)
     iota(T.JF[:, 8:28], [[4, 20]], 0, 0)
     iota(T.JF[:, 28:56], [[4, 28]], 208, 0)
@@ -143,8 +151,8 @@ def rank_program(g, core, T, topo):
             tok = affine(ap, T.NIL[:, 0:n], value, deps=[t_nil])
         return tok
 
-    t_ab = put(coefficients("AL", 0) + coefficients("BE", 1))
-    ga = coefficients("GA", 2)
+    coef = coefficients("AL", 0) + coefficients("BE", 1) + coefficients("GA", 2)
+    put(coef[:20])
     t_pu = vcopy(T.PU[:], T.PO[:], [t_po])
     for i, m in ((1, 15), (2, 12), (3, 12), (4, 3), (5, 1)):
         ts(T.LI[:, i:i + 1], T.LI[:, 0:1], m, Op.bitwise_and, deps=[t_li])
@@ -159,26 +167,25 @@ def rank_program(g, core, T, topo):
     t_lan2 = ts(T.LAN2[:, 2:4], T.LANE[:, 5:7], 319.5, Op.mult, -159.5, Op.add)
     lane, l4, l1, b320 = (T.LANE[:, i:i + 1] for i in (1, 2, 3, 4))
     t_tjb = ts(T.TJB[:], T.C16[:], lane, Op.add, float(PAD), Op.add, [t_c16, t_l1])
+    shift = float(PAD + 4 * 288)
     ts(T.Z4[:], T.C16[:, 20:28], l4, Op.add)
-    t_cz = ts(T.CZ[:], T.C16[:, 20:28], l4, Op.add, 2.0, Op.add)
-    for b in range(4):
-        t_eh = quant("EH", 128 * b, 128 * b + 128, T.ED[:, 3 - b:515 - b], [t_ed])
+    t_cz = ts(T.CZ[:], T.C16[:, 20:28], l4, Op.add, 2.0 - shift / 2, Op.add)
     t_qu = quant("QU", 0, 128, T.UT[:], [du])
     t_us = run("a", lambda q: q.activation(T.UUs[:], T.QUs[:].indirect(T.PU[:]), Fn.Copy), [t_qu, t_pu])
     t_uc = run("v", lambda q: q.tensor_copy(T.UU[:].bitcast(dt.uint32), T.QU[:].bitcast(dt.uint32).indirect(T.PU[:])), [t_qu, t_pu])
-    t_edb = acopy(T.EDB[:], T.ED[:], [t_ed], scale=64.0)
-    put(ga[:6])
+    t_ab = put(coef[20:34])
 
     def a_constants():
-        put(ga[6:])
+        eb = acopy(T.EDB[:], T.ED[:], [t_ed], scale=64.0)
+        put(coef[34:])
         affine(T.TP[:], T.C16[:, 0:20], lane, deps=[t_c16, t_tjb, t_lan2, t_jf])
         affine(T.JF[:, 0:8], T.JF[:, 0:8], lane)
         affine(T.JF[:, 8:56], T.JF[:, 8:56], l1)
         j = affine(T.JF[:, 56:76], T.JF[:, 56:76], lane)
         affine(T.TN[:], T.TP[:], 0.0, -1.0, [j])
         for lo, hi, i in ((0, 8, 0), (8, 56, 1), (56, 76, 0)):
-            e = affine(T.EP[:, lo:hi], T.JF[:, lo:hi], T.LAN2[:, 2 + i:3 + i], T.LAN2[:, i:i + 1], [j])
-        return [e], j
+            e = affine(T.EP[:, lo:hi], T.JF[:, lo:hi], T.LAN2[:, 2 + i:3 + i], T.LAN2[:, i:i + 1])
+        return [e], j, eb
 
     CK, FV, SMT, WA, WO = T.CK, T.FV, T.SM, T.WA, T.WO
     C4, K4, fv = CK[:, 0:1], CK[:, 1:2], SMT[:, 0:1]
@@ -187,7 +194,7 @@ def rank_program(g, core, T, topo):
         i = SCOL[name]
         return FV[:, i:i + 1] if i < NF else T.S4[:, i:i + 1]
 
-    def lists(last, t_s, t_const, copies):
+    def lists(last, t_s, t_const, halves):
         o = (56, 76) if last else (0, 56)
         w = o[1] - o[0]
         J, JI, E, P = T.JF[:, o[0]:o[1]], T.JI[:, o[0]:o[1]], T.EP[:, o[0]:o[1]], T.TP[:]
@@ -205,19 +212,18 @@ def rank_program(g, core, T, topo):
         step("m1", lambda d: ts(wa(0), P, sc("ck"), Op.is_ge, sc("n2n"), Op.mult, d), "s4")
         step("fv", lambda d: tt(FV[:], T.FS[:], T.S4[:, 0:NF], Op.add, d), "fs")
         step("m2", lambda d: ts(wa(1), P, sc("c"), Op.is_ge, sc("X1"), Op.mult, d), "s4")
-        step("ge", lambda d: ts(SMT[:, 5:6], sc("de"), 0.0, Op.is_ge, deps=d), "fv")
-        step("hm", lambda d: ts(SMT[:, 6:7], sc("de"), 0.0, Op.is_lt, deps=d), "fv")
-        step("gxz", lambda d: ts(SMT[:, 8:10], FV[:, SCOL["X"]:SCOL["Z"] + 1], SMT[:, 5:6], Op.mult, deps=d), "ge")
-        copies(2)
+        step("m4x", lambda d: ts(wa(3), P, sc("cpk"), Op.is_ge, sc("k2n"), Op.mult, d), "s4")
+        t_hf = halves()
         step("w", lambda d: affine(wa(6), P, sc("tau"), 2.0, d), "fv")
-        step("e1", lambda d: affine(wo(4), J, SMT[:, 9:10], SMT[:, 8:9], d), "gxz")
-        step("e2", lambda d: affine(wo(5), E, 0.0, SMT[:, 6:7], d), "hm")
-        copies(4)
+        step("q", lambda d: affine(wo(4), J, sc("Z"), sc("X"), d), "fv")
+        for b in range(4):
+            step("f%d" % b, lambda d: acopy(T.PL[:, 432 * b:432 * b + 320], bank(b, 0, 320), [t_hf[b]]))
+            if b < 2:
+                step("p%d" % b, lambda d: acopy(T.FP[:, 320 * b:320 * b + 320], bank(b, 0, 320)))
         ops_a = [
-            ("m4x", lambda d: ts(wa(3), P, sc("cpk"), Op.is_ge, sc("k2n"), Op.mult, d), "s4"),
-            ("a1", lambda d: tt(wa(8), wa(0), T.TN[:], Op.add, d), "m1"),
             ("RB", lambda d: ts(SMT[:, 2:4], FV[:, 0:2], sc("c"), Op.max, deps=d), "fv"),
             ("r2", lambda d: ts(wa(5), P, sc("R1"), Op.is_lt, deps=d), "fv"),
+            ("a1", lambda d: tt(wa(8), wa(0), T.TN[:], Op.add, d), "m1"),
             ("m3", lambda d: ts(wa(2), P, SMT[:, 3:4], Op.is_ge, sc("n2n"), Op.mult, d), "RB"),
             ("r1", lambda d: ts(wa(4), P, SMT[:, 2:3], Op.is_ge, deps=d), "RB"),
             ("a2", lambda d: tt(wa(9), wa(1), wa(2), Op.add, d), "m2", "m3"),
@@ -230,9 +236,9 @@ def rank_program(g, core, T, topo):
         ]
         ops_o = [
             ("t", lambda d: ts(wo(0), J, sc("m4"), Op.subtract, 0.0, Op.max, d), "fv"),
-            ("mx", lambda d: tt(SMT[:, 4:5], sc("de"), sc("d2"), Op.max, d), "fv"),
+            ("ma", lambda d: ts(wo(5), J, sc("d2"), Op.add, 320.0, Op.is_ge, d), "fv"),
             ("Q", lambda d: ts(it("OQ"), wo(0), fv, Op.subtract, 1.0 / 3.0, Op.mult, d), "t"),
-            ("mk", lambda d: ts(wo(8), J, SMT[:, 4:5], Op.add, 320.0, Op.is_ge, d), "mx"),
+            ("mb", lambda d: ts(wo(8), J, sc("de"), Op.add, 320.0, Op.is_ge, d), "fv"),
             ("s5", lambda d: tt(it("OS"), it("OQ"), JI, Op.add, d), "Q"),
             ("b1", lambda d: ts(it("O1"), it("OS"), 1, Op.logical_shift_right, 1, Op.bitwise_and, d), "s5"),
             ("z", lambda d: ts(it("OZ"), it("OS"), 2, Op.logical_shift_right, deps=d), "s5"),
@@ -240,33 +246,37 @@ def rank_program(g, core, T, topo):
             ("sk", lambda d: ts(wo(1), it("O1"), sc("k2"), Op.mult, sc("kh"), Op.add, d), "b1"),
             ("s12", lambda d: ts(wo(2), it("O0"), -2.0, Op.mult, 1.0, Op.add, d), "b0"),
             ("u", lambda d: tt(wo(3), wo(1), it("OZ"), Op.add, d), "sk", "z"),
-            ("p3", lambda d: tt(wo(7), wo(4), wo(5), Op.add, d), "e1", "e2"),
             ("p12", lambda d: tt(wo(6), wo(2), wo(3), Op.mult, d), "s12", "u"),
-            ("df", lambda d: tt(wo(9), wo(7), wo(6), Op.subtract, d), "p3", "p12"),
-            ("dm", lambda d: tt(wo(10), wo(9), wo(8), Op.mult, d), "df", "mk"),
-            ("pl", lambda d: tt(wo(11), wo(10), wo(6), Op.add, d), "dm"),
+            ("da", lambda d: tt(wo(7), E, wo(6), Op.subtract, d), "p12"),
+            ("db", lambda d: tt(wo(9), wo(4), wo(6), Op.subtract, d), "q", "p12"),
+            ("xa", lambda d: tt(wo(10), wo(7), wo(5), Op.mult, d), "da", "ma"),
+            ("xb", lambda d: tt(wo(12), wo(9), wo(8), Op.mult, d), "db", "mb"),
+            ("x1", lambda d: tt(wo(13), wo(10), wo(6), Op.add, d), "xa"),
+            ("pl", lambda d: tt(wo(11), wo(13), wo(12), Op.add, d), "x1", "xb"),
         ]
-        if last:
-            ops_o.append(("LO", lambda d: ts(T.LO[:, 0:20], wo(11), sc("cm"), Op.add, deps=d), "pl"))
-        else:
-            ops_o.append(("LOx", lambda d: ts(T.LO[:, 0:8], WO[:, 704:712], sc("cm"), Op.add, deps=d), "pl"))
-            ops_o.append(("LO", lambda d: ts(T.LO[:, 8:56], WO[:, 712:760], sc("cm"), Op.add, b320, Op.add, d), "pl"))
         na, no = len(ops_a), len(ops_o)
         for j in range(max(na, no)):
-            if j < no:
-                step(*ops_o[j])
             if j < na:
                 step(*ops_a[j])
-        return k["LA"], k["LO"]
+            if j < no:
+                step(*ops_o[j])
 
-    first, rest, tail = [dx], [dx, t_pad0], None
+        def finish():
+            if last:
+                return ts(T.LO[:, 0:20], wo(11), sc("cm"), Op.add, deps=[k["pl"]])
+            ts(T.LO[:, 0:8], WO[:, 704:712], sc("cm"), Op.add, deps=[k["pl"]])
+            return ts(T.LO[:, 8:56], WO[:, 712:760], sc("cm"), Op.add, b320, Op.add)
+
+        return k, finish
+
+    first, low, tail, behind = [dx], [dx, dy, t_pad0], None, None
     for t in range(3):
         X, last = T["X%d" % t], t == 2
         t_qs = quant("QS", 0, 128, X[:, PAD + 320:PAD + 832], first)
         t_s1 = mm(6, 128, "UU", 0, "QS", 0, [t_qs, t_uc, t_us])
         t_s2 = mm(7, 128, "UU", 128, "QS", 0)
         if tail:
-            rest = rest + [tail()]
+            low = low + [tail()]
         t1 = run("v", lambda q: q.tensor_tensor_scan(T.RMC[:], T.NIL[:, 0:65], bank(6, 48, 113), -1e29, Op.add, Op.max), [t_s1, t_nil])
         t2 = run("v", lambda q: q.tensor_tensor_scan(T.RMK[:], T.NIL[:, 0:25], bank(7, 0, 25), -1e29, Op.add, Op.max), [t_s2])
         t3 = ts(T.LTC[:, 0:65], T.RMC[:], T.RMC[:, 64:65], Op.is_lt, 4.0, Op.mult, [t1])
@@ -274,20 +284,22 @@ def rank_program(g, core, T, topo):
         t5 = run("v", lambda q: q.tensor_reduce(C4, T.LTC[:], AxisListType.X, Op.add), [t3, t_lt])
         t6 = run("v", lambda q: q.tensor_reduce(K4, T.LTK[:], AxisListType.X, Op.add), [t4])
         w2 = lambda i: T.W2[:, 8 * i:8 * i + 8]
-        fm, kf = SMT[:, 12:13], SMT[:, 13:14]
+        fm, k8 = SMT[:, 12:13], SMT[:, 13:14]
         t7 = ts(fm, C4, 640.0, Op.is_ge, -1.0, Op.mult, [t5])
         t_l1 = ts(T.L1[:], T.TJB[:, 0:20], C4, Op.add, K4, Op.subtract, [t6, t_tjb])
-        t_b1 = acopy(T.BT[:, 0:320], X[:].indirect(T.L1[:]), [t_l1, t_bt] + rest)
-        t9 = ts(kf, fm, 1.0, Op.add, K4, Op.mult, [t7])
-        t8 = ts(w2(0), T.Z4[:], K4, Op.is_ge, 2.0, Op.mult, [t_cz])
-        t10 = ts(w2(1), T.CZ[:], fm, Op.mult, kf, Op.add, [t9])
-        ts(fv, C4, 640.0, Op.is_lt)
+        t_b1 = acopy(T.BT[:, 0:320], X[:, 0:WIN].indirect(T.L1[:]), [t_l1, t_bt] + low)
+        t9 = ts(k8, K4, 2.0, Op.mult, -shift, Op.add)
+        t10 = ts(w2(1), T.CZ[:], K4, Op.add, fm, Op.mult, [t7, t_cz])
+        t8 = ts(w2(0), T.Z4[:], K4, Op.is_ge, 2.0, Op.mult)
+        tx = ts(w2(4), T.Z4[:], K4, Op.is_ge, k8, Op.mult, [t9])
         t11 = tt(w2(2), w2(0), w2(1), Op.mult, [t8, t10])
+        tb = tt(w2(5), w2(4), T.TJB[:, 20:28], Op.add, [tx])
+        ts(fv, C4, 640.0, Op.is_lt)
+        t12 = tt(w2(3), w2(2), w2(5), Op.add, [t11, tb])
         ts(T.S1[:], T.AL[:], C4, Op.mult, 0.25, Op.mult, [t_ab])
-        t12 = tt(w2(3), w2(2), T.TJB[:, 20:28], Op.add, [t11])
-        t_s = ts(T.S2[:], T.BE[:], K4, Op.mult, 0.25, Op.mult)
         t_l2 = ts(T.L2[:], w2(3), C4, Op.add, K4, Op.subtract, [t12])
-        t_b2 = vcopy(T.BT[:, 320:448], X[:].indirect(T.L2[:]), [t_l2] + rest)
+        t_s = ts(T.S2[:], T.BE[:], K4, Op.mult, 0.25, Op.mult)
+        t_b2 = vcopy(T.BT[:, 320:448], X[:, 0:WIN].indirect(T.L2[:]), [t_l2] + low)
         B, G = "B%d" % t, "G%d" % t
         t_qb = quant(B, 0, 128, T.BT[:], [t_b1, t_b2])
         engines = topo.engines(core, prev)[:8]
@@ -298,107 +310,102 @@ def rank_program(g, core, T, topo):
             g.remote_dma(out, in_, T.sem["arr%d" % t], T.sem.sent, pid, rid, mask)
             total["sent"] = total.get("sent", 0) + len(engines)
         total["arr%d" % t] = 2 * len(topo.engines(nxt, core)[:8])
-        t_qx = quant("QX", 0, 320, X[:, PAD:PAD + 1280], rest)
+        rest = low + ([behind()] if behind else [])
         if t == 0:
             for i in range(3):
                 dma("sy", T["G%d" % i][:, 112:128].bitcast(dt.uint8), T.B0[:, 112:128].bitcast(dt.uint8), "dn", [t_qb])
                 t_gn = dma("sy", T["G%ds" % i][:, 112:128], T.B0s[:, 112:128], "dn")
-            t_con, t_j = a_constants()
+            t_con, t_j, t_edb = a_constants()
             for n in ("X1", "X2"):
-                for o in (0, PAD + 1280):
-                    t_pad = iota(T[n][:, o:o + PAD], [[0, PAD]], 0, 0)
+                t_pad = iota(T[n][:, 128:PAD], [[0, NZ]], 0, 0)
             t_iot = iota(T.IOT[:], [[1, 320]], 0, 0)
+            for b in range(4):
+                t_eh = quant("EH", 128 * b, 128 * b + 128, T.ED[:, 3 - b:515 - b], [t_ed])
             for b in range(4):
                 t_eb = quant("EB", 128 * b, 128 * b + 128, T.EDB[:, 3 - b:515 - b], [t_edb])
             t_con.append(vcopy(T.JI[:], T.JF[:], [t_j]))
-        t_hf = [mm(b, 320, "EH", 128 * b, "QX", 0, [t_qx, t_eh]) for b in range(4)]
-        done = {}
 
-        def copies(n):
-            for b in range(n - 2, n):
-                done[b] = acopy(T.PL[:, 432 * b:432 * b + 320], bank(b, 0, 320), [t_hf[b]])
-                if b < 2:
-                    done[b] = acopy(T.FP[:, 320 * b:320 * b + 320], bank(b, 0, 320))
+        def halves(X=X, rest=rest, t_eh=t_eh):
+            qx = quant("QX", 0, 320, X[:, PAD:XW], rest)
+            return [mm(b, 320, "EH", 128 * b, "QX", 0, [qx, t_eh]) for b in range(4)]
 
-        t_la, t_lo = lists(last, [t_s], t_con, copies)
+        k, finish = lists(last, [t_s], t_con, halves)
         for b in range(2):
-            mm(RBANK[0][b], 160, "EB", 128 * b, "QX", 0, [done[b], t_eb], stop=False)
+            part(0, b, "EB", "QX", [k["p%d" % b], t_eb], True, False)
         if t == 0:
             t_qv = quant("QV", 0, 128, T.VT[:], [dv])
         if last:
+            t_lo = finish()
             t_lor = run("a", lambda q: q.activation(T.LOR[:], T.IOT[:].indirect(T.LO[:, 0:20]), Fn.Copy), [t_lo, t_iot])
             dma("sy", T.lo[:], T.LOR[0:128:16, :], "out", [t_lor])
         t_g = {}
-        for b, bk in ((0, 4), (2, 5), (1, 6), (3, 7)):
-            t_g[b] = mm(bk, 128, "EH", 128 * b, G, 0, [("arr%d" % t, total["arr%d" % t]), t_gn])
+        for b in (0, 2, 1, 3):
+            t_g[b] = mm(GBANK[b], 128, "EH", 128 * b, G, 0, [("arr%d" % t, total["arr%d" % t]), t_gn])
         win = lambda b: T.PL[:, 432 * b:432 * b + 432]
         late = lambda b: T.PL[:, 432 * b + 320:432 * b + 432]
-        la = lambda h: T.LA[:, 10 * h:10 * h + 10]
-        zt = lambda b, h: T.ZT[:, 640 * h + b:640 * h + 640:4]
-        fp = lambda b, h: T.FP[:, 320 * b + 160 * h:320 * b + 160 * h + 160]
-        ab = lambda b, h: T.AB[:, 320 * (b - 2) + 160 * h:320 * (b - 2) + 160 * h + 160]
-        t_c, t_a = {}, {}
-        t_c[2] = acopy(late(2), bank(5, 0, 112), [t_g[2]])
-        t_a[2, 0] = acopy(ab(2, 0), win(2).indirect(la(0)), [t_la, t_c[2]])
-        t_c[3] = acopy(late(3), bank(7, 0, 112), [t_g[3]])
-        t_a[3, 0] = acopy(ab(3, 0), win(3).indirect(la(0)), [t_c[3]])
-        t_a[2, 1] = acopy(ab(2, 1), win(2).indirect(la(1)))
-        t_a[3, 1] = acopy(ab(3, 1), win(3).indirect(la(1)))
-        t_c[0] = vcopy(late(0), bank(4, 0, 112), [t_g[0]])
-        tt(zt(0, 0), win(0).indirect(la(0)), fp(0, 0), Op.add, [t_c[0], done[3], t_la])
-        t_c[1] = vcopy(late(1), bank(6, 0, 112), [t_g[1]])
-        tt(zt(1, 0), win(1).indirect(la(0)), fp(1, 0), Op.add, [t_c[1]])
-        mm(RBANK[0][2], 160, "EB", 256, "QX", 0, [t_c[0]], stop=False)
-        mm(RBANK[0][3], 160, "EB", 384, "QX", 0, [t_c[2]], stop=False)
-        mm(RBANK[1][0], 160, "EB", 0, "QX", 160, [t_c[1]], stop=False)
-        mm(RBANK[1][1], 160, "EB", 128, "QX", 160, [t_c[3]], stop=False)
-        tt(zt(2, 0), bank(2, 0, 160), ab(2, 0), Op.add, [t_a[2, 0]])
-        t_z = tt(zt(3, 0), bank(3, 0, 160), ab(3, 0), Op.add, [t_a[3, 0]])
-        t_qz = quant("QZ", 0, 160, T.ZT[:, 0:640], [t_z])
-        tt(zt(0, 1), win(0).indirect(la(1)), fp(0, 1), Op.add)
-        tt(zt(1, 1), win(1).indirect(la(1)), fp(1, 1), Op.add)
-        t_z2 = tt(zt(2, 1), bank(2, 160, 320), ab(2, 1), Op.add, [t_a[2, 1]])
-        t_z3 = tt(zt(3, 1), bank(3, 160, 320), ab(3, 1), Op.add, [t_a[3, 1]])
-        t_qz2 = quant("QZ", 160, 320, T.ZT[:, 640:1280], [t_z3])
-        yp = lambda b, h: T.YP[:, 320 * b + 160 * h:320 * b + 160 * h + 160]
-        t_r = [mm(RBANK[0][b], 160, "QW", 128 * b, "QZ", 0, [t_qz, dw], start=False) for b in range(4)]
-        mm(2, 160, "EB", 256, "QX", 160, [t_z2], stop=False)
-        mm(3, 160, "EB", 384, "QX", 160, [t_z3], stop=False)
-        t_r2 = [mm(RBANK[1][b], 160, "QW", 128 * b, "QZ", 160, [t_qz2], start=False) for b in range(4)]
-        new = [acopy(yp(b, 0), bank(RBANK[0][b], 0, 160), [t_r[b]], scale=0.03125) for b in range(4)]
+        la = lambda h: T.LA[:, PART[h][0] // 16:PART[h][1] // 16]
+        zt = lambda b, h: T.ZT[:, 4 * PART[h][0] + b:4 * PART[h][1]:4]
+        at = lambda buf, b, h: buf[:, 320 * b + PART[h][0]:320 * b + PART[h][1]]
+        t_c, t_a, t_z = {}, {}, {}
+        for h in range(2):
+            for b in (2, 3):
+                if h == 0:
+                    t_c[b] = acopy(late(b), bank(GBANK[b], 0, 112), [t_g[b]])
+                t_a[b, h] = acopy(at(T.AB, b, h), win(b).indirect(la(h)), [k["LA"], t_c[b]])
+        for h in range(2):
+            for b in (0, 1):
+                if h == 0:
+                    t_c[b] = vcopy(late(b), bank(GBANK[b], 0, 112), [t_g[b]])
+                tt(zt(b, h), win(b).indirect(la(h)), at(T.FP, b, h), Op.add, [t_c[b], k["LA"], k["f3"]])
+            if h == 0:
+                part(0, 2, "EB", "QX", [t_c[0]], True, False)
+                part(0, 3, "EB", "QX", [t_c[2]], True, False)
+                part(1, 0, "EB", "QX", [t_c[1]], True, False)
+                part(1, 1, "EB", "QX", [t_c[3]], True, False)
+            for b in (2, 3):
+                t_z[b, h] = tt(zt(b, h), bank(b, *PART[h]), at(T.AB, b, h), Op.add, [t_a[b, h]] + ([t_z["pre", b]] if h else []))
+                if h == 0:
+                    t_z["pre", b] = part(1, b, "EB", "QX", [t_z[b, 0]], True, False)
+            lo, hi = PART[h]
+            t_z[h] = quant("QZ", lo, hi, T.ZT[:, 4 * lo:4 * hi], [t_z[3, h]])
+        t_r = [[part(h, b, "QW", "QZ", [t_z[h], dw], False, True) for b in range(4)] for h in range(2)]
+        new = [acopy(at(T.YP, b, 0), bank(RBANK[0][b], 0, 192), [t_r[0][b]], scale=0.03125) for b in range(4)]
+        if not last:
+            t_lo = finish()
         XN, YP, LO = T["X%d" % (t + 1)], T.YP, T.LO
         for b in range(4):
-            src, copy = bank(RBANK[1][b], 0, 160), (vcopy, acopy)[b % 2]
+            src, copy = bank(RBANK[1][b], 0, 128), (vcopy, acopy)[b % 2]
             if b % 2 == 0:
-                ty = ts(yp(b, 1), src, 0.03125, Op.mult, deps=[t_r2[b]])
+                ty = ts(at(YP, b, 1), src, 0.03125, Op.mult, deps=[t_r[1][b]])
             else:
-                ty = acopy(yp(b, 1), src, [t_r2[b]], scale=0.03125)
-            plane, deps = YP[:, 320 * b:320 * b + 320], [ty, new[b], t_lo]
+                ty = acopy(at(YP, b, 1), src, [t_r[1][b]], scale=0.03125)
+            window, deps = YP[:, 320 * b:320 * b + 320], [ty, new[b], t_lo]
             new.append(ty)
             if last:
-                new.append(copy(XN[:, b:640:4], plane.indirect(LO[:, 0:10]), deps))
+                new.append(copy(XN[:, b:768:4], window.indirect(LO[:, 0:12]), deps))
             else:
-                new.append(copy(XN[:, PAD + 320 + b:PAD + 832:4], plane.indirect(LO[:, 0:8]), deps))
+                new.append(copy(XN[:, PAD + 320 + b:PAD + 832:4], window.indirect(LO[:, 0:8]), deps))
         first = list(new)
         if not last:
-            r1 = acopy(XN[:, PAD + 832:PAD + 1280], YP[:].indirect(LO[:, 28:56]), new)
+            r1 = acopy(XN[:, 0:128], YP[:].indirect(LO[:, 48:56]), new)
             r2 = acopy(XN[:, PAD + 128:PAD + 320], YP[:].indirect(LO[:, 16:28]))
             tail = lambda XN=XN, new=new: vcopy(XN[:, PAD:PAD + 128], T.YP[:].indirect(T.LO[:, 8:16]), new)
-            rest = new + [r1, r2, t_pad]
+            behind = lambda XN=XN: acopy(XN[:, PAD + 832:XW], T.YP[:].indirect(T.LO[:, 28:56]))
+            low = new + [r1, r2, t_pad]
 
     second = []
     for b in range(4):
-        second.append((vcopy, acopy)[b % 2](XN[:, 640 + b:1280:4], YP[:, 320 * b:320 * b + 320].indirect(LO[:, 10:20]), new))
+        second.append((vcopy, acopy)[b % 2](XN[:, 768 + b:1280:4], YP[:, 320 * b:320 * b + 320].indirect(LO[:, 12:20]), new))
         if b == 0:
-            t_q0 = quant("QF", 0, 160, XN[:, 0:640], first)
-    t_q1 = quant("QF", 160, 320, XN[:, 640:1280], second)
-    t_y0 = mm(2, 160, "QV", 0, "QF", 0, [t_q0, t_qv])
-    t_y1 = mm(3, 160, "QV", 0, "QF", 160, [t_q1])
-    t_o0 = acopy(T.YO[:, 0:160], bank(2, 0, 160), [t_y0])
-    dma("a", T.y[:, 0:160], T.YO[:, 0:160], "out", [t_o0])
+            t_q0 = quant("QF", 0, 192, XN[:, 0:768], first)
+    t_q1 = quant("QF", 192, 320, XN[:, 768:1280], second)
+    t_y0 = mm(2, 192, "QV", 0, "QF", 0, [t_q0, t_qv])
+    t_y1 = mm(3, 128, "QV", 0, "QF", 192, [t_q1])
+    t_o0 = acopy(T.YO[:, 0:192], bank(2, 0, 192), [t_y0])
+    dma("a", T.y[:, 0:192], T.YO[:, 0:192], "out", [t_o0])
     dma("sy", T.oc[:], T.QF[:].bitcast(dt.uint8), "out", [t_q0, t_q1])
-    for k in range(4):
-        dma("a" if k < 2 else "sy", T.osc[4 * k:4 * k + 4, :], T.QFs[32 * k:32 * k + 4, :], "out", [t_q0, t_q1])
-    t_o1 = vcopy(T.YO[:, 160:320], bank(3, 0, 160), [t_y1])
-    dma("sy", T.y[:, 160:320], T.YO[:, 160:320], "out", [t_o1])
+    t_o1 = vcopy(T.YO[:, 192:320], bank(3, 0, 128), [t_y1])
+    for i in range(4):
+        dma("a" if i < 2 else "sy", T.osc[4 * i:4 * i + 4, :], T.QFs[32 * i:32 * i + 4, :], "out", [t_q0, t_q1])
+    dma("sy", T.y[:, 192:320], T.YO[:, 192:320], "out", [t_o1])
     wait("gc", list(total.items()))

import numpy as np
from concourse.mybir import AluOpType as Op, AxisListType, ActivationFunctionType as Fn, dt

NZ = 256
PAD = 128 + NZ
XW = PAD + 1280
WIN = PAD + 832
PART = ((0, 192), (192, 320))
FCOLS = [
    ("R0", (0, 2, 0), (2, -2, 0)), ("B1", (2, 2, -320), (0, 0, 0)),
    ("R1", (2, 2, -320), (-2, -2, 1320)), ("tau", (-1, -3, -319), (-2, 2, 640)),
    ("m4", (-4, -4, 1280), (8, 0, -1280)), ("de", (1, -2, 0), (-2, 0, 320)),
    ("d2", (-2, 4, 0), (4, 0, -640)), ("X", (0, 0, -1), (0, 0, 2)), ("Z", (-1, 0, 319.5), (0, 0, -319)),
]
NCOLS = [
    ("ck", (1, -1, 0)), ("base", (1, -1, 319)), ("n2n", (1, 1, -320)), ("cpk", (1, 1, 0)), ("c", (1, 0, 0)),
    ("cm", (1, 0, -0.5)), ("X1", (-1, 1, 320)), ("k2n", (0, -2, 0)), ("k2", (0, 2, 0)), ("kh", (0, -1, 0.5)),
]
NF, NN = len(FCOLS), len(NCOLS)
NL = 2 * NF + NN
LIN = [a for _, a, _ in FCOLS] + [a for _, a in NCOLS] + [b for _, _, b in FCOLS]
SCOL = {n: i for i, n in enumerate([n for n, _, _ in FCOLS] + [n for n, _ in NCOLS])}

F8, U8, BF, F32, I32, U16 = "float8_e4m3fn_x4", "uint8", "bfloat16", "float32", "int32", "uint16"
SCRATCH = {"PS": ("psum", [128, 4096], F32)}
for _n, _w in (("X0", XW), ("X1", XW), ("X2", XW), ("X3", 1280), ("UT", 512), ("VT", 512), ("BT", 512), ("ZT", 1280), ("PL", 1728),
               ("FP", 640), ("AB", 1280), ("YP", 1280), ("ED", 516), ("EDB", 516), ("HALF", 516)):
    SCRATCH[_n] = ("sbuf", [128, _w], BF)
for _n, _w in (("QU", 128), ("UU", 256), ("QV", 128), ("QW", 512), ("EH", 512), ("EB", 512), ("QS", 128), ("QX", 320), ("QZ", 320),
               ("QF", 320), ("B0", 128), ("B1", 128), ("B2", 128), ("G0", 128), ("G1", 128), ("G2", 128)):
    SCRATCH[_n] = ("sbuf", [128, _w], F8)
    SCRATCH[_n + "s"] = ("sbuf", [128, _w], U8)
for _n, _w in (("C16", 28), ("TJB", 28), ("TP", 20), ("TN", 20), ("Z4", 8), ("CZ", 8), ("LANE", 7), ("LAN2", 4), ("JF", 76), ("EP", 76), ("NIL", 68),
               ("AL", NL), ("BE", NL), ("GA", NL), ("IOT", 320), ("LOR", 320), ("YO", 320), ("RMC", 65), ("RMK", 25), ("LTC", 66), ("LTK", 26),
               ("CK", 2), ("S1", NL), ("S2", NL), ("S3", NL), ("S4", NL), ("FS", NF), ("FV", NF), ("SM", 16), ("W2", 64), ("WA", 320), ("WO", 1024)):
    SCRATCH[_n] = ("sbuf", [128, _w], F32)
for _n, _w in (("LI", 7), ("JI", 76), ("PO", 16), ("OQ", 56), ("OS", 56), ("O0", 56), ("O1", 56), ("OZ", 56)):
    SCRATCH[_n] = ("sbuf", [128, _w], I32)
for _n, _w in (("PU", 16), ("L1", 20), ("L2", 8), ("LA", 20), ("LO", 56)):
    SCRATCH[_n] = ("sbuf", [128, _w], U16)
SEMAPHORES = ["v", "a", "te", "gc", "dx", "dy", "du", "dv", "dw", "dn", "out", "arr0", "arr1", "arr2", "sent"]
RBANK = ((0, 1, 4, 5), (6, 7, 2, 3))
GBANK = (4, 6, 5, 7)


def rank_program(g, core, T, topo):
    rank = T.rank_of(core)
    if rank is None:
        return
    N = len(T.cores)
    prev, nxt = T.cores[(rank - 1) % N], T.cores[(rank + 1) % N]
    queue = {"v": g.vector, "a": g.scalar, "te": g.tensor, "gc": g, "sy": g.sync}
    total, known = {}, {}

    def wait(q, deps):
        need = {}
        for s, n in deps:
            need[s] = max(need.get(s, 0), n)
        for s, n in need.items():
            if known.get((q, s), 0) < n:
                queue[q].wait_ge(T.sem[s], n)
                known[(q, s)] = n

    def run(q, fn, deps=()):
        wait(q, deps)
        ins = fn(queue[q])
        total[q] = total.get(q, 0) + 1
        ins.then_inc(T.sem[q], 1)
        return (q, total[q])

    def dma(q, out, in_, sem, deps=()):
        wait(q, deps)
        queue[q].dma_start(out, in_).then_inc(T.sem[sem], 16)
        total[sem] = total.get(sem, 0) + 16
        return (sem, total[sem])

    def ts(out, in0, s1, op0, s2=None, op1=None, deps=()):
        if op1 is None:
            return run("v", lambda q: q.tensor_scalar(out, in0, s1, None, op0), deps)
        return run("v", lambda q: q.tensor_scalar(out, in0, s1, s2, op0, op1), deps)

    def tt(out, a, b, op, deps=()):
        return run("v", lambda q: q.tensor_tensor(out, a, b, op), deps)

    def vcopy(out, in_, deps=()):
        return run("v", lambda q: q.tensor_copy(out, in_), deps)

    def acopy(out, in_, deps=(), scale=1.0):
        return run("a", lambda q: q.activation(out, in_, Fn.Copy, scale=scale), deps)

    def affine(out, in_, bias, scale=1.0, deps=()):
        return run("a", lambda q: q.activation(out, in_, Fn.Identity, bias=bias, scale=scale), deps)

    def quant(name, lo, hi, in_, deps=()):
        return run("v", lambda q: q.quantize_mx(T[name][:, lo:hi], T[name + "s"][:, lo:hi], in_), deps)

    def mm(bank, n, w, wlo, x, xlo, deps=(), start=True, stop=True):
        return run("te", lambda q: q.matmul_mx(T.PS[:, 512 * bank:512 * bank + n], T[w][:, wlo:wlo + 128], T[w + "s"][:, wlo:wlo + 128],
                                               T[x][:, xlo:xlo + n], T[x + "s"][:, xlo:xlo + n], start, stop), deps)

    def part(h, b, w, x, deps, start, stop):
        lo, hi = PART[h]
        return mm(RBANK[h][b], hi - lo, w, 128 * b, x, lo, deps, start, stop)

    def bank(b, lo, hi):
        return T.PS[:, 512 * b + lo:512 * b + hi]

    def fill(ap, value):
        return run("v", lambda q: q.memset(ap, value))

    def iota(ap, pattern, base, cm, flag=True):
        if flag:
            return run("gc", lambda q: q.iota(ap, pattern, base, cm, allow_small_or_imprecise_dtypes=True))
        return run("gc", lambda q: q.iota(ap, pattern, base, cm))

    dx = dma("sy", T.X0[:, PAD:XW], T.x[:], "dx")
    du = dma("a", T.UT[:], T.u[:], "du")
    dy = dma("sy", T.X0[:, 0:128], T.x[:, 1152:1280], "dy")
    dma("sy", T.QW[:].bitcast(dt.uint8), T.wc[:], "dw")
    dw = dma("sy", T.QWs[:], T.ws[:], "dw")
    dv = dma("sy", T.VT[:], T.v[:], "dv")

    t_po = iota(T.PO[:], [[1, 2], [16, 8]], 0, 0, flag=False)
    t_li = iota(T.LI[:, 0:1], [[0, 1]], 0, 1, flag=False)
    t_c16 = iota(T.C16[:], [[16, 28]], 0, 0)
    fill(T.NIL[:], 0.0)
    fill(T.AL[:], 0.0)
    fill(T.BE[:], 0.0)
    t_nil = fill(T.GA[:], 0.0)
    t_half = fill(T.HALF[:], 0.5)
    t_ed = run("gc", lambda q: q.affine_select(T.ED[:], T.HALF[:], [[-1, 516]], Op.is_equal, 0.0, 3, 4), [t_half])
    t_pad0 = iota(T.X0[:, 128:PAD], [[0, NZ]], 0, 0)
    iota(T.JF[:, 0:8], [[16, 8]], 80, 0)
    iota(T.JF[:, 8:28], [[4, 20]], 0, 0)
    iota(T.JF[:, 28:56], [[4, 28]], 208, 0)
    t_jf = iota(T.JF[:, 56:76], [[16, 20]], 0, 0)

    def coefficients(name, i):
        runs, j = [], 0
        while j < NL:
            e = j
            while e < NL and LIN[e][i] == LIN[j][i]:
                e += 1
            if LIN[j][i] != 0:
                runs.append((T[name][:, j:e], float(LIN[j][i]), e - j))
            j = e
        return runs

    def put(runs):
        for ap, value, n in runs:
            tok = affine(ap, T.NIL[:, 0:n], value, deps=[t_nil])
        return tok

    coef = coefficients("AL", 0) + coefficients("BE", 1) + coefficients("GA", 2)
    put(coef[:20])
    t_pu = vcopy(T.PU[:], T.PO[:], [t_po])
    for i, m in ((1, 15), (2, 12), (3, 12), (4, 3), (5, 1)):
        ts(T.LI[:, i:i + 1], T.LI[:, 0:1], m, Op.bitwise_and, deps=[t_li])
    t_l6 = ts(T.LI[:, 6:7], T.LI[:, 0:1], 2, Op.logical_shift_right, 1, Op.bitwise_and)
    fill(T.LTC[:, 65:66], 512.0)
    t_lt = fill(T.LTK[:, 25:26], 320.0)
    t_lane = vcopy(T.LANE[:], T.LI[:], [t_l6])
    t_bt = fill(T.BT[:], 0.0)
    t_l1 = ts(T.LANE[:, 3:4], T.LANE[:, 2:3], 0.25, Op.mult, deps=[t_lane])
    ts(T.LANE[:, 4:5], T.LANE[:, 4:5], 320.0, Op.mult)
    ts(T.LAN2[:, 0:2], T.LANE[:, 5:7], -1.0, Op.mult, 0.5, Op.add)
    t_lan2 = ts(T.LAN2[:, 2:4], T.LANE[:, 5:7], 319.5, Op.mult, -159.5, Op.add)
    lane, l4, l1, b320 = (T.LANE[:, i:i + 1] for i in (1, 2, 3, 4))
    t_tjb = ts(T.TJB[:], T.C16[:], lane, Op.add, float(PAD), Op.add, [t_c16, t_l1])
    shift = float(PAD + 4 * 288)
    ts(T.Z4[:], T.C16[:, 20:28], l4, Op.add)
    t_cz = ts(T.CZ[:], T.C16[:, 20:28], l4, Op.add, 2.0 - shift / 2, Op.add)
    t_qu = quant("QU", 0, 128, T.UT[:], [du])
    t_us = run("a", lambda q: q.activation(T.UUs[:], T.QUs[:].indirect(T.PU[:]), Fn.Copy), [t_qu, t_pu])
    t_uc = run("v", lambda q: q.tensor_copy(T.UU[:].bitcast(dt.uint32), T.QU[:].bitcast(dt.uint32).indirect(T.PU[:])), [t_qu, t_pu])
    t_ab = put(coef[20:34])

    def a_constants():
        eb = acopy(T.EDB[:], T.ED[:], [t_ed], scale=64.0)
        put(coef[34:])
        affine(T.TP[:], T.C16[:, 0:20], lane, deps=[t_c16, t_tjb, t_lan2, t_jf])
        affine(T.JF[:, 0:8], T.JF[:, 0:8], lane)
        affine(T.JF[:, 8:56], T.JF[:, 8:56], l1)
        j = affine(T.JF[:, 56:76], T.JF[:, 56:76], lane)
        affine(T.TN[:], T.TP[:], 0.0, -1.0, [j])
        for lo, hi, i in ((0, 8, 0), (8, 56, 1), (56, 76, 0)):
            e = affine(T.EP[:, lo:hi], T.JF[:, lo:hi], T.LAN2[:, 2 + i:3 + i], T.LAN2[:, i:i + 1])
        return [e], j, eb

    CK, FV, SMT, WA, WO = T.CK, T.FV, T.SM, T.WA, T.WO
    C4, K4, fv = CK[:, 0:1], CK[:, 1:2], SMT[:, 0:1]

    def sc(name):
        i = SCOL[name]
        return FV[:, i:i + 1] if i < NF else T.S4[:, i:i + 1]

    def lists(last, t_s, t_const, halves):
        o = (56, 76) if last else (0, 56)
        w = o[1] - o[0]
        J, JI, E, P = T.JF[:, o[0]:o[1]], T.JI[:, o[0]:o[1]], T.EP[:, o[0]:o[1]], T.TP[:]
        wa = lambda i: WA[:, 20 * i:20 * i + 20]
        wo = lambda i: WO[:, 64 * i:64 * i + w]
        it = lambda n: T[n][:, 0:w]
        k = {"s": t_s, "con": t_const}

        def step(name, fn, *deps):
            k[name] = fn([x for d in deps for x in (k[d] if isinstance(k[d], list) else [k[d]])])

        step("s3", lambda d: tt(T.S3[:], T.S1[:], T.GA[:], Op.add, d), "s", "con")
        step("s4", lambda d: tt(T.S4[:], T.S3[:], T.S2[:], Op.add, d), "s3")
        step("fs", lambda d: ts(T.FS[:], T.S4[:, NF + NN:NL], fv, Op.mult, deps=d), "s4")
        step("m1", lambda d: ts(wa(0), P, sc("ck"), Op.is_ge, sc("n2n"), Op.mult, d), "s4")
        step("fv", lambda d: tt(FV[:], T.FS[:], T.S4[:, 0:NF], Op.add, d), "fs")
        step("m2", lambda d: ts(wa(1), P, sc("c"), Op.is_ge, sc("X1"), Op.mult, d), "s4")
        step("m4x", lambda d: ts(wa(3), P, sc("cpk"), Op.is_ge, sc("k2n"), Op.mult, d), "s4")
        t_hf = halves()
        step("w", lambda d: affine(wa(6), P, sc("tau"), 2.0, d), "fv")
        step("q", lambda d: affine(wo(4), J, sc("Z"), sc("X"), d), "fv")
        for b in range(4):
            step("f%d" % b, lambda d: acopy(T.PL[:, 432 * b:432 * b + 320], bank(b, 0, 320), [t_hf[b]]))
            if b < 2:
                step("p%d" % b, lambda d: acopy(T.FP[:, 320 * b:320 * b + 320], bank(b, 0, 320)))
        ops_a = [
            ("RB", lambda d: ts(SMT[:, 2:4], FV[:, 0:2], sc("c"), Op.max, deps=d), "fv"),
            ("r2", lambda d: ts(wa(5), P, sc("R1"), Op.is_lt, deps=d), "fv"),
            ("a1", lambda d: tt(wa(8), wa(0), T.TN[:], Op.add, d), "m1"),
            ("m3", lambda d: ts(wa(2), P, SMT[:, 3:4], Op.is_ge, sc("n2n"), Op.mult, d), "RB"),
            ("r1", lambda d: ts(wa(4), P, SMT[:, 2:3], Op.is_ge, deps=d), "RB"),
            ("a2", lambda d: tt(wa(9), wa(1), wa(2), Op.add, d), "m2", "m3"),
            ("rw", lambda d: tt(wa(7), wa(5), wa(4), Op.mult, d), "r2", "r1"),
            ("a4", lambda d: tt(wa(11), wa(8), wa(9), Op.add, d), "a1", "a2"),
            ("rv", lambda d: tt(wa(10), wa(6), wa(7), Op.mult, d), "w", "rw"),
            ("a6", lambda d: tt(wa(12), wa(11), wa(3), Op.add, d), "a4", "m4x"),
            ("a5", lambda d: tt(wa(13), wa(10), wa(12), Op.add, d), "rv", "a6"),
            ("LA", lambda d: ts(T.LA[:], wa(13), sc("base"), Op.add, deps=d), "a5"),
        ]
        ops_o = [
            ("t", lambda d: ts(wo(0), J, sc("m4"), Op.subtract, 0.0, Op.max, d), "fv"),
            ("ma", lambda d: ts(wo(5), J, sc("d2"), Op.add, 320.0, Op.is_ge, d), "fv"),
            ("Q", lambda d: ts(it("OQ"), wo(0), fv, Op.subtract, 1.0 / 3.0, Op.mult, d), "t"),
            ("mb", lambda d: ts(wo(8), J, sc("de"), Op.add, 320.0, Op.is_ge, d), "fv"),
            ("s5", lambda d: tt(it("OS"), it("OQ"), JI, Op.add, d), "Q"),
            ("b1", lambda d: ts(it("O1"), it("OS"), 1, Op.logical_shift_right, 1, Op.bitwise_and, d), "s5"),
            ("z", lambda d: ts(it("OZ"), it("OS"), 2, Op.logical_shift_right, deps=d), "s5"),
            ("b0", lambda d: ts(it("O0"), it("OS"), 1, Op.bitwise_and, deps=d), "s5"),
            ("sk", lambda d: ts(wo(1), it("O1"), sc("k2"), Op.mult, sc("kh"), Op.add, d), "b1"),
            ("s12", lambda d: ts(wo(2), it("O0"), -2.0, Op.mult, 1.0, Op.add, d), "b0"),
            ("u", lambda d: tt(wo(3), wo(1), it("OZ"), Op.add, d), "sk", "z"),
            ("p12", lambda d: tt(wo(6), wo(2), wo(3), Op.mult, d), "s12", "u"),
            ("da", lambda d: tt(wo(7), E, wo(6), Op.subtract, d), "p12"),
            ("db", lambda d: tt(wo(9), wo(4), wo(6), Op.subtract, d), "q", "p12"),
            ("xa", lambda d: tt(wo(10), wo(7), wo(5), Op.mult, d), "da", "ma"),
            ("xb", lambda d: tt(wo(12), wo(9), wo(8), Op.mult, d), "db", "mb"),
            ("x1", lambda d: tt(wo(13), wo(10), wo(6), Op.add, d), "xa"),
            ("pl", lambda d: tt(wo(11), wo(13), wo(12), Op.add, d), "x1", "xb"),
        ]
        na, no = len(ops_a), len(ops_o)
        for j in range(max(na, no)):
            if j < na:
                step(*ops_a[j])
            if j < no:
                step(*ops_o[j])

        def finish():
            if last:
                return ts(T.LO[:, 0:20], wo(11), sc("cm"), Op.add, deps=[k["pl"]])
            ts(T.LO[:, 0:8], WO[:, 704:712], sc("cm"), Op.add, deps=[k["pl"]])
            return ts(T.LO[:, 8:56], WO[:, 712:760], sc("cm"), Op.add, b320, Op.add)

        return k, finish

    first, low, tail, behind = [dx], [dx, dy, t_pad0], None, None
    for t in range(3):
        X, last = T["X%d" % t], t == 2
        t_qs = quant("QS", 0, 128, X[:, PAD + 320:PAD + 832], first)
        t_s1 = mm(6, 128, "UU", 0, "QS", 0, [t_qs, t_uc, t_us])
        t_s2 = mm(7, 128, "UU", 128, "QS", 0)
        if tail:
            low = low + [tail()]
        t1 = run("v", lambda q: q.tensor_tensor_scan(T.RMC[:], T.NIL[:, 0:65], bank(6, 48, 113), -1e29, Op.add, Op.max), [t_s1, t_nil])
        t2 = run("v", lambda q: q.tensor_tensor_scan(T.RMK[:], T.NIL[:, 0:25], bank(7, 0, 25), -1e29, Op.add, Op.max), [t_s2])
        t3 = ts(T.LTC[:, 0:65], T.RMC[:], T.RMC[:, 64:65], Op.is_lt, 4.0, Op.mult, [t1])
        t4 = ts(T.LTK[:, 0:25], T.RMK[:], T.RMK[:, 24:25], Op.is_lt, 4.0, Op.mult, [t2])
        t5 = run("v", lambda q: q.tensor_reduce(C4, T.LTC[:], AxisListType.X, Op.add), [t3, t_lt])
        t6 = run("v", lambda q: q.tensor_reduce(K4, T.LTK[:], AxisListType.X, Op.add), [t4])
        w2 = lambda i: T.W2[:, 8 * i:8 * i + 8]
        fm, k8 = SMT[:, 12:13], SMT[:, 13:14]
        t7 = ts(fm, C4, 640.0, Op.is_ge, -1.0, Op.mult, [t5])
        t_l1 = ts(T.L1[:], T.TJB[:, 0:20], C4, Op.add, K4, Op.subtract, [t6, t_tjb])
        t_b1 = acopy(T.BT[:, 0:320], X[:, 0:WIN].indirect(T.L1[:]), [t_l1, t_bt] + low)
        t9 = ts(k8, K4, 2.0, Op.mult, -shift, Op.add)
        t10 = ts(w2(1), T.CZ[:], K4, Op.add, fm, Op.mult, [t7, t_cz])
        t8 = ts(w2(0), T.Z4[:], K4, Op.is_ge, 2.0, Op.mult)
        tx = ts(w2(4), T.Z4[:], K4, Op.is_ge, k8, Op.mult, [t9])
        t11 = tt(w2(2), w2(0), w2(1), Op.mult, [t8, t10])
        tb = tt(w2(5), w2(4), T.TJB[:, 20:28], Op.add, [tx])
        ts(fv, C4, 640.0, Op.is_lt)
        t12 = tt(w2(3), w2(2), w2(5), Op.add, [t11, tb])
        ts(T.S1[:], T.AL[:], C4, Op.mult, 0.25, Op.mult, [t_ab])
        t_l2 = ts(T.L2[:], w2(3), C4, Op.add, K4, Op.subtract, [t12])
        t_s = ts(T.S2[:], T.BE[:], K4, Op.mult, 0.25, Op.mult)
        t_b2 = vcopy(T.BT[:, 320:448], X[:, 0:WIN].indirect(T.L2[:]), [t_l2] + low)
        B, G = "B%d" % t, "G%d" % t
        t_qb = quant(B, 0, 128, T.BT[:], [t_b1, t_b2])
        engines = topo.engines(core, prev)[:8]
        mask = sum(1 << e for e in engines)
        rid, pid = topo.addr(prev)[:2]
        wait("gc", [t_qb])
        for out, in_ in ((T[G][:, 0:112].bitcast(dt.uint8), T[B][:, 0:112].bitcast(dt.uint8)), (T[G + "s"][:, 0:112], T[B + "s"][:, 0:112])):
            g.remote_dma(out, in_, T.sem["arr%d" % t], T.sem.sent, pid, rid, mask)
            total["sent"] = total.get("sent", 0) + len(engines)
        total["arr%d" % t] = 2 * len(topo.engines(nxt, core)[:8])
        rest = low + ([behind()] if behind else [])
        if t == 0:
            for i in range(3):
                dma("sy", T["G%d" % i][:, 112:128].bitcast(dt.uint8), T.B0[:, 112:128].bitcast(dt.uint8), "dn", [t_qb])
                t_gn = dma("sy", T["G%ds" % i][:, 112:128], T.B0s[:, 112:128], "dn")
            t_con, t_j, t_edb = a_constants()
            for n in ("X1", "X2"):
                t_pad = iota(T[n][:, 128:PAD], [[0, NZ]], 0, 0)
            t_iot = iota(T.IOT[:], [[1, 320]], 0, 0)
            for b in range(4):
                t_eh = quant("EH", 128 * b, 128 * b + 128, T.ED[:, 3 - b:515 - b], [t_ed])
            for b in range(4):
                t_eb = quant("EB", 128 * b, 128 * b + 128, T.EDB[:, 3 - b:515 - b], [t_edb])
            t_con.append(vcopy(T.JI[:], T.JF[:], [t_j]))

        def halves(X=X, rest=rest, t_eh=t_eh):
            qx = quant("QX", 0, 320, X[:, PAD:XW], rest)
            return [mm(b, 320, "EH", 128 * b, "QX", 0, [qx, t_eh]) for b in range(4)]

        k, finish = lists(last, [t_s], t_con, halves)
        for b in range(2):
            part(0, b, "EB", "QX", [k["p%d" % b], t_eb], True, False)
        if t == 0:
            t_qv = quant("QV", 0, 128, T.VT[:], [dv])
        if last:
            t_lo = finish()
            t_lor = run("a", lambda q: q.activation(T.LOR[:], T.IOT[:].indirect(T.LO[:, 0:20]), Fn.Copy), [t_lo, t_iot])
            dma("sy", T.lo[:], T.LOR[0:128:16, :], "out", [t_lor])
        t_g = {}
        for b in (0, 2, 1, 3):
            t_g[b] = mm(GBANK[b], 128, "EH", 128 * b, G, 0, [("arr%d" % t, total["arr%d" % t]), t_gn])
        win = lambda b: T.PL[:, 432 * b:432 * b + 432]
        late = lambda b: T.PL[:, 432 * b + 320:432 * b + 432]
        la = lambda h: T.LA[:, PART[h][0] // 16:PART[h][1] // 16]
        zt = lambda b, h: T.ZT[:, 4 * PART[h][0] + b:4 * PART[h][1]:4]
        at = lambda buf, b, h: buf[:, 320 * b + PART[h][0]:320 * b + PART[h][1]]
        t_c, t_a, t_z = {}, {}, {}
        for h in range(2):
            for b in (2, 3):
                if h == 0:
                    t_c[b] = acopy(late(b), bank(GBANK[b], 0, 112), [t_g[b]])
                t_a[b, h] = acopy(at(T.AB, b, h), win(b).indirect(la(h)), [k["LA"], t_c[b]])
        for h in range(2):
            for b in (0, 1):
                if h == 0:
                    t_c[b] = vcopy(late(b), bank(GBANK[b], 0, 112), [t_g[b]])
                tt(zt(b, h), win(b).indirect(la(h)), at(T.FP, b, h), Op.add, [t_c[b], k["LA"], k["f3"]])
            if h == 0:
                part(0, 2, "EB", "QX", [t_c[0]], True, False)
                part(0, 3, "EB", "QX", [t_c[2]], True, False)
                part(1, 0, "EB", "QX", [t_c[1]], True, False)
                part(1, 1, "EB", "QX", [t_c[3]], True, False)
            for b in (2, 3):
                t_z[b, h] = tt(zt(b, h), bank(b, *PART[h]), at(T.AB, b, h), Op.add, [t_a[b, h]] + ([t_z["pre", b]] if h else []))
                if h == 0:
                    t_z["pre", b] = part(1, b, "EB", "QX", [t_z[b, 0]], True, False)
            lo, hi = PART[h]
            t_z[h] = quant("QZ", lo, hi, T.ZT[:, 4 * lo:4 * hi], [t_z[3, h]])
        t_r = [[part(h, b, "QW", "QZ", [t_z[h], dw], False, True) for b in range(4)] for h in range(2)]
        new = [acopy(at(T.YP, b, 0), bank(RBANK[0][b], 0, 192), [t_r[0][b]], scale=0.03125) for b in range(4)]
        if not last:
            t_lo = finish()
        XN, YP, LO = T["X%d" % (t + 1)], T.YP, T.LO
        for b in range(4):
            src, copy = bank(RBANK[1][b], 0, 128), (vcopy, acopy)[b % 2]
            if b % 2 == 0:
                ty = ts(at(YP, b, 1), src, 0.03125, Op.mult, deps=[t_r[1][b]])
            else:
                ty = acopy(at(YP, b, 1), src, [t_r[1][b]], scale=0.03125)
            window, deps = YP[:, 320 * b:320 * b + 320], [ty, new[b], t_lo]
            new.append(ty)
            if last:
                new.append(copy(XN[:, b:768:4], window.indirect(LO[:, 0:12]), deps))
            else:
                new.append(copy(XN[:, PAD + 320 + b:PAD + 832:4], window.indirect(LO[:, 0:8]), deps))
        first = list(new)
        if not last:
            r1 = acopy(XN[:, 0:128], YP[:].indirect(LO[:, 48:56]), new)
            r2 = acopy(XN[:, PAD + 128:PAD + 320], YP[:].indirect(LO[:, 16:28]))
            tail = lambda XN=XN, new=new: vcopy(XN[:, PAD:PAD + 128], T.YP[:].indirect(T.LO[:, 8:16]), new)
            behind = lambda XN=XN: acopy(XN[:, PAD + 832:XW], T.YP[:].indirect(T.LO[:, 28:56]))
            low = new + [r1, r2, t_pad]

    second = []
    for b in range(4):
        second.append((vcopy, acopy)[b % 2](XN[:, 768 + b:1280:4], YP[:, 320 * b:320 * b + 320].indirect(LO[:, 12:20]), new))
        if b == 0:
            t_q0 = quant("QF", 0, 192, XN[:, 0:768], first)
    t_q1 = quant("QF", 192, 320, XN[:, 768:1280], second)
    t_y0 = mm(2, 192, "QV", 0, "QF", 0, [t_q0, t_qv])
    t_y1 = mm(3, 128, "QV", 0, "QF", 192, [t_q1])
    t_o0 = acopy(T.YO[:, 0:192], bank(2, 0, 192), [t_y0])
    dma("a", T.y[:, 0:192], T.YO[:, 0:192], "out", [t_o0])
    dma("sy", T.oc[:], T.QF[:].bitcast(dt.uint8), "out", [t_q0, t_q1])
    t_o1 = vcopy(T.YO[:, 192:320], bank(3, 0, 128), [t_y1])
    for i in range(4):
        dma("a" if i < 2 else "sy", T.osc[4 * i:4 * i + 4, :], T.QFs[32 * i:32 * i + 4, :], "out", [t_q0, t_q1])
    dma("sy", T.y[:, 192:320], T.YO[:, 192:320], "out", [t_o1])
    wait("gc", list(total.items()))
